import numpy as np
import ml_dtypes


def mxq(x, axis, fmt="e4m3"):
    dtype, down = {"e4m3": (ml_dtypes.float8_e4m3fn, 7), "e5m2": (ml_dtypes.float8_e5m2, 14)}[fmt]
    v = np.moveaxis(np.asarray(x, np.float32).astype(ml_dtypes.bfloat16).astype(np.float64), axis, -1)
    blocks = v.reshape(v.shape[:-1] + (-1, 32))
    amax = np.abs(blocks).max(-1, keepdims=True)
    byte = np.maximum(np.where(amax > 0, np.frexp(amax)[1] - 1 + 127, 0) - down, 1)
    scale = np.exp2(byte - 127.0)
    codes = (blocks / scale).astype(np.float32).astype(dtype).astype(np.float64)
    return np.moveaxis((codes * scale).reshape(v.shape), -1, axis)


WIDE = False


def mx_kscale(k):
    if not WIDE:
        return np.ones(k)
    levels = np.array([10, -10, 5, -5, 0])
    if k % 512:
        return np.exp2(np.random.permutation(np.resize(levels, k // 32))).repeat(32)
    a = np.empty((k // 512, 16))
    for p in range(k // 512):
        a[p, :8] = np.random.permutation(np.resize(levels, 8))
        for g in range(8):
            far = levels[np.abs(levels - a[p, g]) >= 10]
            a[p, g + 8] = far[np.random.randint(len(far))]
    return np.exp2(a.ravel()).repeat(32)


def f64(x):
    return np.asarray(x).astype(np.float64)


def striped(idx):
    return np.tile(idx.reshape(-1, 16).T, (8, 1)).astype(np.uint16)


def unstriped(offs):
    return offs[:16].T.reshape(-1).astype(np.int64)


def striped8(idx):
    return np.concatenate([x.reshape(-1, 16).T for x in idx]).astype(np.uint16)


def runs(offs, k):
    lists = np.stack([offs[16 * r : 16 * r + 16].T.reshape(-1) for r in range(8)]).astype(np.int64)
    return lists[np.arange(k) % 512 // 64]


def pack_weight(w):
    k, n = w.shape
    w = f64(np.asarray(w, np.float32).astype(ml_dtypes.bfloat16)).reshape(k // 32, 32, n)
    amax = np.abs(w).max(1)
    byte = np.clip(np.where(amax > 0, np.frexp(amax)[1] - 1 + 127 - 7, 1), 1, 254)
    scaled = (w * np.exp2(127.0 - byte)[:, None, :]).reshape(k, n).astype(np.float32)
    words = np.ascontiguousarray(scaled.reshape(k // 512, 128, 4, n).transpose(0, 1, 3, 2)).astype(ml_dtypes.float8_e4m3fn).view(np.uint8)
    return words, np.ascontiguousarray(byte.astype(np.uint8).reshape(k // 512, 16, n))


def unpack_weight(words, scales):
    g, p, n, _ = words.shape
    vals = np.ascontiguousarray(words).view(ml_dtypes.float8_e4m3fn).astype(np.float64) * np.repeat(np.exp2(scales.astype(np.float64) - 127.0), 8, axis=1)[..., None]
    return vals.transpose(0, 1, 3, 2).reshape(g * 512, n)


E2M1 = np.array([0.0, 0.5, 1.0, 1.5, 2.0, 3.0, 4.0, 6.0, -0.0, -0.5, -1.0, -1.5, -2.0, -3.0, -4.0, -6.0])


def pack_fp4(w):
    k, n = w.shape
    w = f64(np.asarray(w, np.float32).astype(ml_dtypes.bfloat16)).reshape(k // 32, 32, n)
    amax = np.abs(w).max(1)
    mant, ex = np.frexp(amax / 6.0)
    byte = np.clip(np.where(amax > 0, np.where(mant > 0.5, ex, ex - 1) + 127, 1), 1, 254)
    scaled = (w * np.exp2(127.0 - byte)[:, None, :]).reshape(k, n).astype(np.float32)
    c = np.ascontiguousarray(scaled.reshape(k // 512, 128, 4, n).transpose(0, 1, 3, 2)).astype(ml_dtypes.float4_e2m1fn).view(np.uint8) & 0xF
    words = (c[..., 0::2] | (c[..., 1::2] << 4)).reshape(k // 512, 128, 2 * n)
    return np.ascontiguousarray(words), np.ascontiguousarray(byte.astype(np.uint8).reshape(k // 512, 16, n))


def unpack_fp4(words, scales):
    g, _, n = scales.shape
    words = np.ascontiguousarray(words).reshape(g, 128, n, 2)
    nib = np.empty((g, 128, n, 4), np.uint8)
    nib[..., 0::2] = words & 0xF
    nib[..., 1::2] = words >> 4
    vals = E2M1[nib] * np.repeat(np.exp2(scales.astype(np.float64) - 127.0), 8, axis=1)[..., None]
    return vals.transpose(0, 1, 3, 2).reshape(g * 512, n)


def planes(y):
    n, m = y.shape
    v = y.astype(np.float32).astype(ml_dtypes.bfloat16).astype(np.float64).reshape(n // 32, 32, m)
    top = np.abs(v).max(1)
    byte = np.clip(np.where(top > 0, np.frexp(top)[1] - 1 + 127 - 7, 1), 1, 254)
    codes = (v * np.exp2(127.0 - byte)[:, None, :]).reshape(n, m).astype(np.float32).astype(ml_dtypes.float8_e4m3fn).view(np.uint8)
    words = codes.reshape(n // 512, 128, 4, m).transpose(0, 1, 3, 2)
    return np.ascontiguousarray(words), np.ascontiguousarray(byte.astype(np.uint8).reshape(n // 512, 16, m))


K, T, S, N, G, H = 512, 2048, 512, 512, 2048, 512


def setup_inputs():
    n = np.random.standard_normal
    s = mx_kscale(K)[:, None]
    u = mx_kscale(H)
    packed_xT = pack_weight(n((K, T)) * s)
    packed_dT = pack_weight(n((K, G)) / s)
    packed_w1 = pack_fp4(n((H, N)) / np.sqrt(H) / u[:, None])
    return {
        "x_words": packed_xT[0],
        "x_scales": packed_xT[1],
        "d_words": packed_dT[0],
        "d_scales": packed_dT[1],
        "gn": (np.random.uniform(0.5, 1.5, (H, 1)) * u[:, None]).astype(np.float32),
        "w1_words": packed_w1[0],
        "w1_scales": packed_w1[1],
        "offs": striped(np.random.permutation(T)[:S]),
        "k1": striped8(np.random.randint(0, G, (8, H))),
        "k2": striped8(np.random.randint(0, G, (8, H))),
    }


def reference(x_words, x_scales, d_words, d_scales, gn, w1_words, w1_scales, offs, k1, k2):
    d_k1 = unpack_weight(d_words, d_scales)[np.arange(K)[:, None], runs(k1, K)]
    xq = unpack_weight(x_words, x_scales)[:, unstriped(offs)]
    a = 0.0625 * (d_k1.T @ xq)
    d_k2 = unpack_weight(d_words, d_scales)[np.arange(K)[:, None], runs(k2, K)]
    b = 0.0625 * (d_k2.T @ xq)
    z = f64(gn) * np.maximum(a, b)
    out_0 = unpack_fp4(w1_words, w1_scales).T @ mxq(z, 0, "e4m3")
    return (out_0,) + planes(out_0)

@@ -1,0 +1,170 @@
+from contextlib import ExitStack
+
+import concourse.mybir as mybir
+from concourse.masks import make_identity
+
+K, T, S, N, G, H = 512, 2048, 512, 512, 2048, 512
+FLOPS = 2 * K * H * S * 2 + 2 * H * N * S
+
+F32 = mybir.dt.float32
+BF16 = mybir.dt.bfloat16
+I32 = mybir.dt.int32
+U32 = mybir.dt.uint32
+U16 = mybir.dt.uint16
+U8 = mybir.dt.uint8
+FP8X4 = mybir.dt.float8_e4m3fn_x4
+FP4X4 = mybir.dt.float4_e2m1fn_x4
+MAX = mybir.AluOpType.max
+MULT = mybir.AluOpType.mult
+
+P = 128
+PACK = 4
+TOK = 128
+TILES = S // TOK
+
+
+def tile_picked_maxsim_none_po_kernel(
+    tc, x_words, x_scales, d_words, d_scales, gn, w1_words, w1_scales, offs, k1, k2, out_0, out_1, out_2
+):
+    nc = tc.nc
+    with ExitStack() as ctx:
+        keep = ctx.enter_context(tc.tile_pool(name="keep", bufs=1))
+        ring = ctx.enter_context(tc.tile_pool(name="ring", bufs=2))
+        shared = ctx.enter_context(tc.tile_pool(name="shared", bufs=1))
+        psum = ctx.enter_context(tc.psum_pool(name="psum", bufs=2))
+
+        k1_list = keep.tile([P, H // 16], U16)
+        k2_list = keep.tile([P, H // 16], U16)
+        x_list = keep.tile([P, S // 16], U16)
+        d_bytes = keep.tile([P, G], U8, align_bytes=64)
+        x_bytes = keep.tile([P, T], U8, align_bytes=64)
+        d_table = shared.tile([P, G], I32, align_bytes=64, offset=0)
+        x_table = keep.tile([P, T], I32, align_bytes=64)
+        w_raw = keep.tile([P, 2 * N], U8, align_bytes=64)
+        w_rows = keep.tile([P, N], U8, align_bytes=64)
+        gain = keep.tile([P, PACK], F32)
+        planes = keep.tile([P, 2 * H + S], U8, align_bytes=64)
+        ident = keep.tile([P, P], F32)
+
+        nc.gpsimd.memset(w_rows[:].bitcast(I32), 0)
+        nc.gpsimd.memset(planes[:].bitcast(I32), 0)
+
+        nc.sync.dma_start(k1_list[:], k1)
+        nc.scalar.dma_start(d_bytes[:].bitcast(I32), d_scales[0].bitcast(I32).unsqueeze(1).to_broadcast([16, 8, G // 4]))
+        nc.sync.dma_start(k2_list[:], k2)
+        nc.scalar.dma_start(x_bytes[:].bitcast(I32), x_scales[0].bitcast(I32).unsqueeze(1).to_broadcast([16, 8, T // 4]))
+        nc.sync.dma_start(x_list[:], offs)
+        nc.sync.dma_start(x_table[:], x_words[0].rearrange("p c r -> p (c r)").bitcast(I32))
+        nc.sync.dma_start(d_table[:], d_words[0].rearrange("p c r -> p (c r)").bitcast(I32))
+        nc.sync.dma_start(w_raw[:].bitcast(I32), w1_words[0].bitcast(I32))
+        for q in range(4):
+            nc.gpsimd.dma_start(w_rows[32 * q : 32 * q + 4, :].bitcast(I32), w1_scales[0, 4 * q : 4 * q + 4, :].bitcast(I32))
+        nc.scalar.dma_start(gain[:], gn.rearrange("(p t) o -> p (t o)", t=PACK))
+        make_identity(nc, ident[:])
+
+        picked = keep.tile([P, 2 * H + S], U8, align_bytes=64)
+        nc.vector.tensor_copy(picked[:, 0:H], d_bytes[:].indirect(k1_list[:]))
+        nc.vector.tensor_copy(picked[:, H : 2 * H], d_bytes[:].indirect(k2_list[:]))
+        nc.vector.tensor_copy(picked[:, 2 * H :], x_bytes[:].indirect(x_list[:]))
+        for q in range(4):
+            nc.scalar.dma_start(
+                planes[32 * q : 32 * q + 4, :].bitcast(I32), picked[32 * q : 32 * q + 32 : 8, :].bitcast(I32)
+            )
+
+        d1 = keep.tile([P, H], U32, align_bytes=64)
+        d2 = keep.tile([P, H], U32, align_bytes=64)
+        xq = keep.tile([P, S], U32, align_bytes=64)
+        nc.vector.tensor_copy(xq[:], x_table[:].bitcast(U32).indirect(x_list[:]))
+        nc.vector.tensor_copy(d1[:], d_table[:].bitcast(U32).indirect(k1_list[:]))
+        nc.vector.tensor_copy(d2[:], d_table[:].bitcast(U32).indirect(k2_list[:]))
+
+        w_codes = shared.tile([P, 2 * N], U8, align_bytes=64, offset=0)
+        w_plane = shared.tile([P, N], U8, align_bytes=64, offset=2 * N)
+        nc.vector.tensor_copy(
+            w_codes[:].rearrange("p (t m e) -> p t m e", t=PACK, e=2),
+            w_raw[:].rearrange("p (m t e) -> p t m e", t=PACK, e=2),
+        )
+        nc.vector.tensor_copy(
+            w_plane[:].rearrange("p (t m) -> p t m", t=PACK), w_rows[:].rearrange("p (m t) -> p t m", t=PACK)
+        )
+
+        y_codes = keep.tile([P, S], U32, align_bytes=64)
+        y_plane = keep.tile([P, S], U8, align_bytes=64)
+        out_rows = out_0.rearrange("(p t) j -> p t j", t=PACK)
+        out_words = out_1[0].rearrange("p c r -> p (c r)").bitcast(I32)
+
+        a_sb, b_ps, best, turned, z, y_ps, y, y_half = [{} for i in range(8)]
+
+        def tokens(c):
+            return xq[:, TOK * c : TOK * (c + 1)].bitcast(FP8X4), planes[:, 2 * H + TOK * c : 2 * H + TOK * (c + 1)]
+
+        def first(c):
+            a_ps = psum.tile([P, H], F32, name="a_ps")
+            nc.tensor.matmul_mx(a_ps[:], *tokens(c), d1[:].bitcast(FP8X4), planes[:, 0:H], start=True, stop=True)
+            a_sb[c] = ring.tile([P, PACK, P], F32, name="a_sb", bufs=TILES)
+            nc.scalar.copy(a_sb[c][:], a_ps[:].rearrange("j (p t) -> j t p", t=PACK))
+
+        def second(c):
+            b_ps[c] = psum.tile([P, H], F32, name="b_ps")
+            nc.tensor.matmul_mx(b_ps[c][:], *tokens(c), d2[:].bitcast(FP8X4), planes[:, H : 2 * H], start=True, stop=True)
+
+        def larger(c):
+            best[c] = ring.tile([P, PACK, P], F32, name="best")
+            nc.vector.tensor_tensor(best[c][:], b_ps[c][:].rearrange("j (p t) -> j t p", t=PACK), a_sb[c][:], MAX)
+            turned[c] = psum.tile([P, PACK, TOK], F32, name="turned")
+            for t in range(PACK):
+                nc.tensor.transpose(turned[c][:, t, :], best[c][:, t, :], ident[:])
+
+        def weigh(c):
+            z[c] = ring.tile([P, TOK, PACK], BF16, align_bytes=64, name="z")
+            nc.vector.scalar_tensor_tensor(
+                z[c][:],
+                turned[c][:].rearrange("p t j -> p j t"),
+                0.0625,
+                gain[:].unsqueeze(1).to_broadcast([P, TOK, PACK]),
+                MULT,
+                MULT,
+            )
+
+        def values(c):
+            z_codes = ring.tile([P, TOK], U32, align_bytes=64, name="z_codes")
+            z_plane = ring.tile([P, TOK], U8, align_bytes=64, name="z_plane")
+            nc.vector.quantize_mx(z_codes[:].bitcast(FP8X4), z_plane[:], z[c][:].rearrange("p j t -> p (j t)"))
+            y_ps[c] = psum.tile([P, PACK, TOK], F32, name="y_ps")
+            for t in range(PACK):
+                nc.tensor.matmul_mx(
+                    y_ps[c][:, t, :],
+                    w_codes[:, 2 * P * t : 2 * P * (t + 1)].bitcast(FP4X4),
+                    w_plane[:, P * t : P * (t + 1)],
+                    z_codes[:].bitcast(FP8X4),
+                    z_plane[:],
+                    start=True,
+                    stop=True,
+                )
+            cols = slice(TOK * c, TOK * (c + 1))
+            y[c] = ring.tile([P, PACK, TOK], F32, name="y", bufs=TILES)
+            nc.scalar.copy(y[c][:], y_ps[c][:])
+            nc.sync.dma_start(out_rows[:, :, cols], y[c][:])
+            y_half[c] = ring.tile([P, TOK, PACK], BF16, align_bytes=64, name="y_half", bufs=TILES)
+            if c < 2:
+                nc.scalar.copy(y_half[c][:], y_ps[c][:].rearrange("p t j -> p j t"))
+
+        def hand_on(c):
+            cols = slice(TOK * c, TOK * (c + 1))
+            if c >= 2:
+                nc.vector.tensor_copy(y_half[c][:], y[c][:].rearrange("p t j -> p j t"))
+            nc.vector.quantize_mx(
+                y_codes[:, cols].bitcast(FP8X4), y_plane[:, cols], y_half[c][:].rearrange("p j t -> p (j t)")
+            )
+            nc.sync.dma_start(out_words[:, cols], y_codes[:, cols].bitcast(I32))
+
+        stages = [first, second, larger, weigh, values]
+        for step in range(TILES + len(stages) - 1):
+            for depth, stage in enumerate(stages):
+                if 0 <= step - depth < TILES:
+                    stage(step - depth)
+        for c in range(TILES):
+            hand_on(c)
+        for q in range(4):
+            queue = nc.sync if q % 2 == 0 else nc.scalar
+            queue.dma_start(out_2[0, 4 * q : 4 * q + 4, :].bitcast(I32), y_plane[32 * q : 32 * q + 4, :].bitcast(I32))

@@ -31,55 +31,65 @@ def tile_picked_maxsim_none_po_kernel(
         keep = ctx.enter_context(tc.tile_pool(name="keep", bufs=1))
         ring = ctx.enter_context(tc.tile_pool(name="ring", bufs=2))
         shared = ctx.enter_context(tc.tile_pool(name="shared", bufs=1))
-        psum = ctx.enter_context(tc.psum_pool(name="psum", bufs=2))
+        psum = ctx.enter_context(tc.psum_pool(name="psum", bufs=8))
 
         k1_list = keep.tile([P, H // 16], U16)
         k2_list = keep.tile([P, H // 16], U16)
         x_list = keep.tile([P, S // 16], U16)
-        d_bytes = keep.tile([P, G], U8, align_bytes=64)
-        x_bytes = keep.tile([P, T], U8, align_bytes=64)
-        d_table = shared.tile([P, G], I32, align_bytes=64, offset=0)
-        x_table = keep.tile([P, T], I32, align_bytes=64)
+        d_bytes = shared.tile([P, G], U8, align_bytes=64, offset=2048)
+        x_bytes = shared.tile([P, T], U8, align_bytes=64, offset=6144)
+        d_table = shared.tile([P, G], I32, align_bytes=64, offset=8192)
+        x_table = shared.tile([P, T], I32, align_bytes=64, offset=16384)
         w_raw = keep.tile([P, 2 * N], U8, align_bytes=64)
-        w_rows = keep.tile([P, N], U8, align_bytes=64)
-        gain = keep.tile([P, PACK], F32)
-        planes = keep.tile([P, 2 * H + S], U8, align_bytes=64)
+        planes_a = keep.tile([P, H + S], U8, align_bytes=64)
+        planes_b = keep.tile([P, H], U8, align_bytes=64)
         ident = keep.tile([P, P], F32)
 
-        nc.gpsimd.memset(w_rows[:].bitcast(I32), 0)
-        nc.gpsimd.memset(planes[:].bitcast(I32), 0)
-
-        nc.sync.dma_start(k1_list[:], k1)
-        nc.scalar.dma_start(d_bytes[:].bitcast(I32), d_scales[0].bitcast(I32).unsqueeze(1).to_broadcast([16, 8, G // 4]))
-        nc.sync.dma_start(k2_list[:], k2)
-        nc.scalar.dma_start(x_bytes[:].bitcast(I32), x_scales[0].bitcast(I32).unsqueeze(1).to_broadcast([16, 8, T // 4]))
-        nc.sync.dma_start(x_list[:], offs)
-        nc.sync.dma_start(x_table[:], x_words[0].rearrange("p c r -> p (c r)").bitcast(I32))
-        nc.sync.dma_start(d_table[:], d_words[0].rearrange("p c r -> p (c r)").bitcast(I32))
-        nc.sync.dma_start(w_raw[:].bitcast(I32), w1_words[0].bitcast(I32))
-        for q in range(4):
-            nc.gpsimd.dma_start(w_rows[32 * q : 32 * q + 4, :].bitcast(I32), w1_scales[0, 4 * q : 4 * q + 4, :].bitcast(I32))
-        nc.scalar.dma_start(gain[:], gn.rearrange("(p t) o -> p (t o)", t=PACK))
+        nc.gpsimd.memset(d_bytes[:].bitcast(I32), 0)
+        nc.vector.memset(x_bytes[:].bitcast(I32), 0)
+        nc.vector.memset(planes_a[:].bitcast(I32), 0)
+        nc.vector.memset(planes_b[:].bitcast(I32), 0)
         make_identity(nc, ident[:])
 
-        picked = keep.tile([P, 2 * H + S], U8, align_bytes=64)
-        nc.vector.tensor_copy(picked[:, 0:H], d_bytes[:].indirect(k1_list[:]))
-        nc.vector.tensor_copy(picked[:, H : 2 * H], d_bytes[:].indirect(k2_list[:]))
-        nc.vector.tensor_copy(picked[:, 2 * H :], x_bytes[:].indirect(x_list[:]))
-        for q in range(4):
-            nc.scalar.dma_start(
-                planes[32 * q : 32 * q + 4, :].bitcast(I32), picked[32 * q : 32 * q + 32 : 8, :].bitcast(I32)
-            )
+        nc.sync.dma_start(k1_list[:], k1)
+        nc.scalar.dma_start(d_bytes[0:P:8, :].bitcast(I32), d_scales[0].bitcast(I32))
+        nc.sync.dma_start(x_list[:], offs)
+        nc.scalar.dma_start(x_bytes[0:P:8, :].bitcast(I32), x_scales[0].bitcast(I32))
+        nc.sync.dma_start(k2_list[:], k2)
+        nc.sync.dma_start(x_table[:], x_words[0].rearrange("p c r -> p (c r)").bitcast(I32))
+        gain = keep.tile([P, PACK], F32)
+        nc.sync.dma_start(gain[:], gn.rearrange("(p t) o -> p (t o)", t=PACK))
+        nc.sync.dma_start(d_table[:], d_words[0].rearrange("p c r -> p (c r)").bitcast(I32))
+        nc.sync.dma_start(w_raw[:].bitcast(I32), w1_words[0].bitcast(I32))
 
-        d1 = keep.tile([P, H], U32, align_bytes=64)
-        d2 = keep.tile([P, H], U32, align_bytes=64)
-        xq = keep.tile([P, S], U32, align_bytes=64)
+        def place_rows(plane, picked):
+            for q in range(4):
+                nc.sync.dma_start(
+                    plane[32 * q : 32 * q + 4, :].bitcast(I32), picked[32 * q : 32 * q + 32 : 8, :].bitcast(I32)
+                )
+
+        picked_a = keep.tile([P, H + S], U8, align_bytes=64)
+        nc.vector.tensor_copy(picked_a[:, 0:H], d_bytes[:].indirect(k1_list[:]))
+        nc.vector.tensor_copy(picked_a[:, H:], x_bytes[:].indirect(x_list[:]))
+        place_rows(planes_a, picked_a)
+        picked_b = shared.tile([P, H], U8, align_bytes=64, offset=6144)
+        nc.vector.tensor_copy(picked_b[:], d_bytes[:].indirect(k2_list[:]))
+        place_rows(planes_b, picked_b)
+
+        w_rows = shared.tile([P, N], U8, align_bytes=64, offset=2560)
+        nc.gpsimd.memset(w_rows[:].bitcast(I32), 0)
+        for q in range(4):
+            nc.sync.dma_start(w_rows[32 * q : 32 * q + 4, :].bitcast(I32), w1_scales[0, 4 * q : 4 * q + 4, :].bitcast(I32))
+
+        xq = shared.tile([P, S], U32, align_bytes=64, offset=512)
+        d1 = shared.tile([P, H], U32, align_bytes=64, offset=3584)
+        d2 = shared.tile([P, H], U32, align_bytes=64, offset=16384)
         nc.vector.tensor_copy(xq[:], x_table[:].bitcast(U32).indirect(x_list[:]))
         nc.vector.tensor_copy(d1[:], d_table[:].bitcast(U32).indirect(k1_list[:]))
         nc.vector.tensor_copy(d2[:], d_table[:].bitcast(U32).indirect(k2_list[:]))
 
-        w_codes = shared.tile([P, 2 * N], U8, align_bytes=64, offset=0)
-        w_plane = shared.tile([P, N], U8, align_bytes=64, offset=2 * N)
+        w_codes = shared.tile([P, 2 * N], U8, align_bytes=64, offset=8192)
+        w_plane = shared.tile([P, N], U8, align_bytes=64, offset=8192 + 2 * N)
         nc.vector.tensor_copy(
             w_codes[:].rearrange("p (t m e) -> p t m e", t=PACK, e=2),
             w_raw[:].rearrange("p (m t e) -> p t m e", t=PACK, e=2),
@@ -96,27 +106,35 @@ def tile_picked_maxsim_none_po_kernel(
         a_sb, b_ps, best, turned, z, y_ps, y, y_half = [{} for i in range(8)]
 
         def tokens(c):
-            return xq[:, TOK * c : TOK * (c + 1)].bitcast(FP8X4), planes[:, 2 * H + TOK * c : 2 * H + TOK * (c + 1)]
+            return xq[:, TOK * c : TOK * (c + 1)].bitcast(FP8X4), planes_a[:, H + TOK * c : H + TOK * (c + 1)]
 
         def first(c):
-            a_ps = psum.tile([P, H], F32, name="a_ps")
-            nc.tensor.matmul_mx(a_ps[:], *tokens(c), d1[:].bitcast(FP8X4), planes[:, 0:H], start=True, stop=True)
+            a_ps = psum.tile([P, H], F32, name="a_ps", tag="bank")
+            if c == 0:
+                for i in range(2):
+                    nc.tensor.matmul_mx(
+                        a_ps[:], xq[:, 0:TOK].bitcast(FP8X4), picked_a[:, H : H + TOK],
+                        xq[:].bitcast(FP8X4), picked_a[:, H:], start=True, stop=True,
+                    )
+            nc.tensor.matmul_mx(a_ps[:], *tokens(c), d1[:].bitcast(FP8X4), planes_a[:, 0:H], start=True, stop=True)
             a_sb[c] = ring.tile([P, PACK, P], F32, name="a_sb", bufs=TILES)
             nc.scalar.copy(a_sb[c][:], a_ps[:].rearrange("j (p t) -> j t p", t=PACK))
 
         def second(c):
-            b_ps[c] = psum.tile([P, H], F32, name="b_ps")
-            nc.tensor.matmul_mx(b_ps[c][:], *tokens(c), d2[:].bitcast(FP8X4), planes[:, H : 2 * H], start=True, stop=True)
+            b_ps[c] = psum.tile([P, H], F32, name="b_ps", tag="bank")
+            nc.tensor.matmul_mx(b_ps[c][:], *tokens(c), d2[:].bitcast(FP8X4), planes_b[:], start=True, stop=True)
 
         def larger(c):
-            best[c] = ring.tile([P, PACK, P], F32, name="best")
+            best[c] = ring.tile([P, PACK, P], F32, name="best", tag="vec", bufs=16, align_bytes=64)
             nc.vector.tensor_tensor(best[c][:], b_ps[c][:].rearrange("j (p t) -> j t p", t=PACK), a_sb[c][:], MAX)
-            turned[c] = psum.tile([P, PACK, TOK], F32, name="turned")
+
+        def turn(c):
+            turned[c] = psum.tile([P, PACK, TOK], F32, name="turned", tag="bank")
             for t in range(PACK):
                 nc.tensor.transpose(turned[c][:, t, :], best[c][:, t, :], ident[:])
 
         def weigh(c):
-            z[c] = ring.tile([P, TOK, PACK], BF16, align_bytes=64, name="z")
+            z[c] = ring.tile([P, TOK, PACK], BF16, align_bytes=64, name="z", tag="vec", bufs=16)
             nc.vector.scalar_tensor_tensor(
                 z[c][:],
                 turned[c][:].rearrange("p t j -> p j t"),
@@ -127,44 +145,80 @@ def tile_picked_maxsim_none_po_kernel(
             )
 
         def values(c):
-            z_codes = ring.tile([P, TOK], U32, align_bytes=64, name="z_codes")
-            z_plane = ring.tile([P, TOK], U8, align_bytes=64, name="z_plane")
+            z_codes = ring.tile([P, TOK], U32, align_bytes=64, name="z_codes", tag="vec", bufs=16)
+            z_plane = ring.tile([P, TOK], U8, align_bytes=64, name="z_plane", bufs=TILES)
             nc.vector.quantize_mx(z_codes[:].bitcast(FP8X4), z_plane[:], z[c][:].rearrange("p j t -> p (j t)"))
-            y_ps[c] = psum.tile([P, PACK, TOK], F32, name="y_ps")
-            for t in range(PACK):
-                nc.tensor.matmul_mx(
-                    y_ps[c][:, t, :],
-                    w_codes[:, 2 * P * t : 2 * P * (t + 1)].bitcast(FP4X4),
-                    w_plane[:, P * t : P * (t + 1)],
-                    z_codes[:].bitcast(FP8X4),
-                    z_plane[:],
-                    start=True,
-                    stop=True,
-                )
-            cols = slice(TOK * c, TOK * (c + 1))
+
+            def product():
+                bank = psum.tile([P, PACK, TOK], F32, name="y_ps", tag="bank")
+                for t in range(PACK):
+                    nc.tensor.matmul_mx(
+                        bank[:, t, :],
+                        w_codes[:, 2 * P * t : 2 * P * (t + 1)].bitcast(FP4X4),
+                        w_plane[:, P * t : P * (t + 1)],
+                        z_codes[:].bitcast(FP8X4),
+                        z_plane[:],
+                        start=True,
+                        stop=True,
+                    )
+                return bank
+
+            y_ps[c] = product()
+            stored = product() if c == TILES - 1 else y_ps[c]
             y[c] = ring.tile([P, PACK, TOK], F32, name="y", bufs=TILES)
-            nc.scalar.copy(y[c][:], y_ps[c][:])
-            nc.sync.dma_start(out_rows[:, :, cols], y[c][:])
-            y_half[c] = ring.tile([P, TOK, PACK], BF16, align_bytes=64, name="y_half", bufs=TILES)
-            if c < 2:
+            nc.scalar.copy(y[c][:], stored[:])
+            nc.sync.dma_start(out_rows[:, :, TOK * c : TOK * (c + 1)], y[c][:])
+            if c == 0:
+                y_half[c] = ring.tile([P, TOK, PACK], BF16, align_bytes=64, name="y_half0")
                 nc.scalar.copy(y_half[c][:], y_ps[c][:].rearrange("p t j -> p j t"))
+
+        def narrow(c, source):
+            y_half[c] = ring.tile([P, TOK, PACK], BF16, align_bytes=64, name="y_half", tag="vec", bufs=16)
+            nc.vector.tensor_copy(y_half[c][:], source[:].rearrange("p t j -> p j t"))
 
         def hand_on(c):
             cols = slice(TOK * c, TOK * (c + 1))
-            if c >= 2:
-                nc.vector.tensor_copy(y_half[c][:], y[c][:].rearrange("p t j -> p j t"))
             nc.vector.quantize_mx(
                 y_codes[:, cols].bitcast(FP8X4), y_plane[:, cols], y_half[c][:].rearrange("p j t -> p (j t)")
             )
+
+        def store_codes(h):
+            cols = slice(S // 2 * h, S // 2 * (h + 1))
             nc.sync.dma_start(out_words[:, cols], y_codes[:, cols].bitcast(I32))
 
-        stages = [first, second, larger, weigh, values]
-        for step in range(TILES + len(stages) - 1):
-            for depth, stage in enumerate(stages):
-                if 0 <= step - depth < TILES:
-                    stage(step - depth)
-        for c in range(TILES):
-            hand_on(c)
+        first(0)
+        first(1)
+        second(0)
+        second(1)
+        first(2)
+        second(2)
+        larger(0)
+        turn(0)
+        first(3)
+        second(3)
+        larger(1)
+        turn(1)
+        larger(2)
+        turn(2)
+        weigh(0)
+        larger(3)
+        values(0)
+        turn(3)
+        weigh(1)
+        weigh(2)
+        values(1)
+        values(2)
+        weigh(3)
+        values(3)
+        hand_on(0)
+        narrow(1, y[1])
+        narrow(3, y_ps[3])
+        narrow(2, y[2])
+        hand_on(1)
+        store_codes(0)
+        hand_on(3)
+        hand_on(2)
+        store_codes(1)
         for q in range(4):
-            queue = nc.sync if q % 2 == 0 else nc.scalar
+            queue = nc.scalar if q < 3 else nc.sync
             queue.dma_start(out_2[0, 4 * q : 4 * q + 4, :].bitcast(I32), y_plane[32 * q : 32 * q + 4, :].bitcast(I32))

@@ -21,6 +21,10 @@ P = 128
 PACK = 4
 TOK = 128
 TILES = S // TOK
+D_BYTES = 1536
+X_BYTES = D_BYTES + G + 1536
+X_TABLE = X_BYTES + T
+D_TABLE = X_TABLE + 4 * T
 
 
 def tile_picked_maxsim_none_po_kernel(
@@ -36,31 +40,29 @@ def tile_picked_maxsim_none_po_kernel(
         k1_list = keep.tile([P, H // 16], U16)
         k2_list = keep.tile([P, H // 16], U16)
         x_list = keep.tile([P, S // 16], U16)
-        d_bytes = shared.tile([P, G], U8, align_bytes=64, offset=2048)
-        x_bytes = shared.tile([P, T], U8, align_bytes=64, offset=6144)
-        d_table = shared.tile([P, G], I32, align_bytes=64, offset=8192)
-        x_table = shared.tile([P, T], I32, align_bytes=64, offset=16384)
-        w_raw = keep.tile([P, 2 * N], U8, align_bytes=64)
+        gain = keep.tile([P, PACK], F32)
         planes_a = keep.tile([P, H + S], U8, align_bytes=64)
         planes_b = keep.tile([P, H], U8, align_bytes=64)
         ident = keep.tile([P, P], F32)
 
-        nc.gpsimd.memset(d_bytes[:].bitcast(I32), 0)
-        nc.vector.memset(x_bytes[:].bitcast(I32), 0)
+        d_bytes = shared.tile([P, G], U8, align_bytes=64, offset=D_BYTES)
+        x_bytes = shared.tile([P, T], U8, align_bytes=64, offset=X_BYTES)
+        x_table = shared.tile([P, T], I32, align_bytes=64, offset=X_TABLE)
+        d_table = shared.tile([P, G], I32, align_bytes=64, offset=D_TABLE)
+        w_raw = keep.tile([P, 2 * N], U8, align_bytes=64)
         nc.vector.memset(planes_a[:].bitcast(I32), 0)
         nc.vector.memset(planes_b[:].bitcast(I32), 0)
         make_identity(nc, ident[:])
 
         nc.sync.dma_start(k1_list[:], k1)
-        nc.scalar.dma_start(d_bytes[0:P:8, :].bitcast(I32), d_scales[0].bitcast(I32))
+        nc.sync.dma_start(d_bytes[:].bitcast(I32), d_scales[0].bitcast(I32).unsqueeze(1).to_broadcast([16, 8, G // 4]))
         nc.sync.dma_start(x_list[:], offs)
-        nc.scalar.dma_start(x_bytes[0:P:8, :].bitcast(I32), x_scales[0].bitcast(I32))
+        nc.sync.dma_start(x_bytes[:].bitcast(I32), x_scales[0].bitcast(I32).unsqueeze(1).to_broadcast([16, 8, T // 4]))
         nc.sync.dma_start(k2_list[:], k2)
         nc.sync.dma_start(x_table[:], x_words[0].rearrange("p c r -> p (c r)").bitcast(I32))
-        gain = keep.tile([P, PACK], F32)
-        nc.sync.dma_start(gain[:], gn.rearrange("(p t) o -> p (t o)", t=PACK))
         nc.sync.dma_start(d_table[:], d_words[0].rearrange("p c r -> p (c r)").bitcast(I32))
         nc.sync.dma_start(w_raw[:].bitcast(I32), w1_words[0].bitcast(I32))
+        nc.scalar.dma_start(gain[:], gn.rearrange("(p t) o -> p (t o)", t=PACK))
 
         def place_rows(plane, picked):
             for q in range(4):
@@ -72,24 +74,24 @@ def tile_picked_maxsim_none_po_kernel(
         nc.vector.tensor_copy(picked_a[:, 0:H], d_bytes[:].indirect(k1_list[:]))
         nc.vector.tensor_copy(picked_a[:, H:], x_bytes[:].indirect(x_list[:]))
         place_rows(planes_a, picked_a)
-        picked_b = shared.tile([P, H], U8, align_bytes=64, offset=6144)
+        picked_b = shared.tile([P, H], U8, align_bytes=64, offset=X_BYTES)
         nc.vector.tensor_copy(picked_b[:], d_bytes[:].indirect(k2_list[:]))
         place_rows(planes_b, picked_b)
 
-        w_rows = shared.tile([P, N], U8, align_bytes=64, offset=2560)
+        w_rows = shared.tile([P, N], U8, align_bytes=64, offset=D_BYTES + 512)
         nc.gpsimd.memset(w_rows[:].bitcast(I32), 0)
         for q in range(4):
             nc.sync.dma_start(w_rows[32 * q : 32 * q + 4, :].bitcast(I32), w1_scales[0, 4 * q : 4 * q + 4, :].bitcast(I32))
 
-        xq = shared.tile([P, S], U32, align_bytes=64, offset=512)
-        d1 = shared.tile([P, H], U32, align_bytes=64, offset=3584)
-        d2 = shared.tile([P, H], U32, align_bytes=64, offset=16384)
+        xq = shared.tile([P, S], U32, align_bytes=64, offset=0)
+        d1 = shared.tile([P, H], U32, align_bytes=64, offset=D_BYTES + 1536)
+        d2 = shared.tile([P, H], U32, align_bytes=64, offset=X_TABLE)
         nc.vector.tensor_copy(xq[:], x_table[:].bitcast(U32).indirect(x_list[:]))
         nc.vector.tensor_copy(d1[:], d_table[:].bitcast(U32).indirect(k1_list[:]))
         nc.vector.tensor_copy(d2[:], d_table[:].bitcast(U32).indirect(k2_list[:]))
 
-        w_codes = shared.tile([P, 2 * N], U8, align_bytes=64, offset=8192)
-        w_plane = shared.tile([P, N], U8, align_bytes=64, offset=8192 + 2 * N)
+        w_codes = shared.tile([P, 2 * N], U8, align_bytes=64, offset=D_TABLE)
+        w_plane = shared.tile([P, N], U8, align_bytes=64, offset=D_TABLE + 2 * N)
         nc.vector.tensor_copy(
             w_codes[:].rearrange("p (t m e) -> p t m e", t=PACK, e=2),
             w_raw[:].rearrange("p (m t e) -> p t m e", t=PACK, e=2),

@@ -4,7 +4,7 @@ import concourse.mybir as mybir
 from concourse.masks import make_identity
 
 K, T, S, N, G, H = 512, 2048, 512, 512, 2048, 512
-FLOPS = 2 * K * H * S * 2 + 2 * H * N * S
+FLOPS = 2 * (2 * K * H * S) + 2 * H * N * S
 
 F32 = mybir.dt.float32
 BF16 = mybir.dt.bfloat16
@@ -19,12 +19,15 @@ MULT = mybir.AluOpType.mult
 
 P = 128
 PACK = 4
+QUADS = 4
+BLOCK = 8
 TOK = 128
 TILES = S // TOK
-D_BYTES = 1536
-X_BYTES = D_BYTES + G + 1536
-X_TABLE = X_BYTES + T
-D_TABLE = X_TABLE + 4 * T
+HALF = S // 2
+BANKS = 8
+WARM_UP = 2
+VECTOR_MADE = 21
+LATE = 5
 
 
 def tile_picked_maxsim_none_po_kernel(
@@ -33,69 +36,85 @@ def tile_picked_maxsim_none_po_kernel(
     nc = tc.nc
     with ExitStack() as ctx:
         keep = ctx.enter_context(tc.tile_pool(name="keep", bufs=1))
-        ring = ctx.enter_context(tc.tile_pool(name="ring", bufs=2))
         shared = ctx.enter_context(tc.tile_pool(name="shared", bufs=1))
-        psum = ctx.enter_context(tc.psum_pool(name="psum", bufs=8))
+        psum = ctx.enter_context(tc.psum_pool(name="psum", bufs=BANKS))
+
+        def vector_made(name, shape, dtype):
+            return keep.tile(shape, dtype, align_bytes=64, name=name, tag="vector_made", bufs=VECTOR_MADE)
+
+        def late(name, shape, dtype):
+            return keep.tile(shape, dtype, align_bytes=64, name=name, tag="late", bufs=LATE)
+
+        def bank(name, shape):
+            return psum.tile(shape, F32, name=name, tag="bank")
 
         k1_list = keep.tile([P, H // 16], U16)
         k2_list = keep.tile([P, H // 16], U16)
         x_list = keep.tile([P, S // 16], U16)
-        gain = keep.tile([P, PACK], F32)
-        planes_a = keep.tile([P, H + S], U8, align_bytes=64)
-        planes_b = keep.tile([P, H], U8, align_bytes=64)
         ident = keep.tile([P, P], F32)
+        d_bytes = shared.tile([P, G], U8, align_bytes=64, offset=0)
+        x_bytes = shared.tile([P, T], U8, align_bytes=64, offset=G)
+        plane_a = keep.tile([P, H + S], U8, align_bytes=64)
 
-        d_bytes = shared.tile([P, G], U8, align_bytes=64, offset=D_BYTES)
-        x_bytes = shared.tile([P, T], U8, align_bytes=64, offset=X_BYTES)
-        x_table = shared.tile([P, T], I32, align_bytes=64, offset=X_TABLE)
-        d_table = shared.tile([P, G], I32, align_bytes=64, offset=D_TABLE)
-        w_raw = keep.tile([P, 2 * N], U8, align_bytes=64)
-        nc.vector.memset(planes_a[:].bitcast(I32), 0)
-        nc.vector.memset(planes_b[:].bitcast(I32), 0)
+        nc.vector.memset(d_bytes[:].bitcast(I32), 0)
+        nc.vector.memset(x_bytes[:].bitcast(I32), 0)
+        nc.vector.memset(plane_a[:].bitcast(I32), 0)
+        plane_b = late("plane_b", [P, H], U8)
+        nc.vector.memset(plane_b[:].bitcast(I32), 0)
         make_identity(nc, ident[:])
 
         nc.sync.dma_start(k1_list[:], k1)
-        nc.sync.dma_start(d_bytes[:].bitcast(I32), d_scales[0].bitcast(I32).unsqueeze(1).to_broadcast([16, 8, G // 4]))
+        nc.sync.dma_start(d_bytes[0:P:BLOCK, :].bitcast(I32), d_scales[0].bitcast(I32))
         nc.sync.dma_start(x_list[:], offs)
-        nc.sync.dma_start(x_bytes[:].bitcast(I32), x_scales[0].bitcast(I32).unsqueeze(1).to_broadcast([16, 8, T // 4]))
+        nc.sync.dma_start(x_bytes[0:P:BLOCK, :].bitcast(I32), x_scales[0].bitcast(I32))
         nc.sync.dma_start(k2_list[:], k2)
-        nc.sync.dma_start(x_table[:], x_words[0].rearrange("p c r -> p (c r)").bitcast(I32))
+        d_table = late("d_table", [P, G], I32)
         nc.sync.dma_start(d_table[:], d_words[0].rearrange("p c r -> p (c r)").bitcast(I32))
+        w_raw = late("w_raw", [P, 2 * N], U8)
         nc.sync.dma_start(w_raw[:].bitcast(I32), w1_words[0].bitcast(I32))
-        nc.scalar.dma_start(gain[:], gn.rearrange("(p t) o -> p (t o)", t=PACK))
+        x_table = late("x_table", [P, T], I32)
+        nc.sync.dma_start(x_table[:], x_words[0].rearrange("p c r -> p (c r)").bitcast(I32))
+        gain = late("gain", [P, PACK], F32)
+        nc.sync.dma_start(gain[:], gn.rearrange("(p t) o -> p (t o)", t=PACK))
 
         def place_rows(plane, picked):
-            for q in range(4):
+            for q in range(QUADS):
                 nc.sync.dma_start(
-                    plane[32 * q : 32 * q + 4, :].bitcast(I32), picked[32 * q : 32 * q + 32 : 8, :].bitcast(I32)
+                    plane[32 * q : 32 * q + 4, :].bitcast(I32), picked[32 * q : 32 * q + 32 : BLOCK, :].bitcast(I32)
                 )
 
-        picked_a = keep.tile([P, H + S], U8, align_bytes=64)
+        picked_a = vector_made("picked_a", [P, H + S], U8)
         nc.vector.tensor_copy(picked_a[:, 0:H], d_bytes[:].indirect(k1_list[:]))
         nc.vector.tensor_copy(picked_a[:, H:], x_bytes[:].indirect(x_list[:]))
-        place_rows(planes_a, picked_a)
-        picked_b = shared.tile([P, H], U8, align_bytes=64, offset=X_BYTES)
+        place_rows(plane_a, picked_a)
+        picked_b = shared.tile([P, H], U8, align_bytes=64, offset=G)
         nc.vector.tensor_copy(picked_b[:], d_bytes[:].indirect(k2_list[:]))
-        place_rows(planes_b, picked_b)
+        place_rows(plane_b, picked_b)
 
-        w_rows = shared.tile([P, N], U8, align_bytes=64, offset=D_BYTES + 512)
+        w_rows = shared.tile([P, N], U8, align_bytes=64, offset=0)
         nc.gpsimd.memset(w_rows[:].bitcast(I32), 0)
-        for q in range(4):
+        for q in range(QUADS):
             nc.sync.dma_start(w_rows[32 * q : 32 * q + 4, :].bitcast(I32), w1_scales[0, 4 * q : 4 * q + 4, :].bitcast(I32))
 
-        xq = shared.tile([P, S], U32, align_bytes=64, offset=0)
-        d1 = shared.tile([P, H], U32, align_bytes=64, offset=D_BYTES + 1536)
-        d2 = shared.tile([P, H], U32, align_bytes=64, offset=X_TABLE)
-        nc.vector.tensor_copy(xq[:], x_table[:].bitcast(U32).indirect(x_list[:]))
-        nc.vector.tensor_copy(d1[:], d_table[:].bitcast(U32).indirect(k1_list[:]))
-        nc.vector.tensor_copy(d2[:], d_table[:].bitcast(U32).indirect(k2_list[:]))
+        x_codes = {}
 
-        w_codes = shared.tile([P, 2 * N], U8, align_bytes=64, offset=D_TABLE)
-        w_plane = shared.tile([P, N], U8, align_bytes=64, offset=D_TABLE + 2 * N)
+        def pick_tokens(h):
+            x_codes[h] = vector_made("x_codes", [P, HALF], U32)
+            columns = slice(HALF // 16 * h, HALF // 16 * (h + 1))
+            nc.vector.tensor_copy(x_codes[h][:], x_table[:].bitcast(U32).indirect(x_list[:, columns]))
+
+        d1_codes = vector_made("d1_codes", [P, H], U32)
+        nc.vector.tensor_copy(d1_codes[:], d_table[:].bitcast(U32).indirect(k1_list[:]))
+        w_codes = vector_made("w_codes", [P, 2 * N], U8)
         nc.vector.tensor_copy(
             w_codes[:].rearrange("p (t m e) -> p t m e", t=PACK, e=2),
             w_raw[:].rearrange("p (m t e) -> p t m e", t=PACK, e=2),
         )
+        pick_tokens(0)
+        d2_codes = vector_made("d2_codes", [P, H], U32)
+        nc.vector.tensor_copy(d2_codes[:], d_table[:].bitcast(U32).indirect(k2_list[:]))
+        pick_tokens(1)
+        w_plane = vector_made("w_plane", [P, N], U8)
         nc.vector.tensor_copy(
             w_plane[:].rearrange("p (t m) -> p t m", t=PACK), w_rows[:].rearrange("p (m t) -> p t m", t=PACK)
         )
@@ -104,39 +123,45 @@ def tile_picked_maxsim_none_po_kernel(
         y_plane = keep.tile([P, S], U8, align_bytes=64)
         out_rows = out_0.rearrange("(p t) j -> p t j", t=PACK)
         out_words = out_1[0].rearrange("p c r -> p (c r)").bitcast(I32)
-
         a_sb, b_ps, best, turned, z, y_ps, y, y_half = [{} for i in range(8)]
 
         def tokens(c):
-            return xq[:, TOK * c : TOK * (c + 1)].bitcast(FP8X4), planes_a[:, H + TOK * c : H + TOK * (c + 1)]
+            start = TOK * c % HALF
+            codes = x_codes[TOK * c // HALF][:, start : start + TOK].bitcast(FP8X4)
+            return codes, plane_a[:, H + TOK * c : H + TOK * (c + 1)]
 
-        def first(c):
-            a_ps = psum.tile([P, H], F32, name="a_ps", tag="bank")
+        def score_a(c):
+            a_ps = bank("a_ps", [P, H])
             if c == 0:
-                for i in range(2):
+                for i in range(WARM_UP):
                     nc.tensor.matmul_mx(
-                        a_ps[:], xq[:, 0:TOK].bitcast(FP8X4), picked_a[:, H : H + TOK],
-                        xq[:].bitcast(FP8X4), picked_a[:, H:], start=True, stop=True,
+                        a_ps[:],
+                        d1_codes[:, 0:P].bitcast(FP8X4),
+                        picked_a[:, 0:P],
+                        d1_codes[:].bitcast(FP8X4),
+                        picked_a[:, 0:H],
+                        start=True,
+                        stop=True,
                     )
-            nc.tensor.matmul_mx(a_ps[:], *tokens(c), d1[:].bitcast(FP8X4), planes_a[:, 0:H], start=True, stop=True)
-            a_sb[c] = ring.tile([P, PACK, P], F32, name="a_sb", bufs=TILES)
+            nc.tensor.matmul_mx(a_ps[:], *tokens(c), d1_codes[:].bitcast(FP8X4), plane_a[:, 0:H], start=True, stop=True)
+            a_sb[c] = keep.tile([P, PACK, P], F32, name="a_sb", bufs=TILES)
             nc.scalar.copy(a_sb[c][:], a_ps[:].rearrange("j (p t) -> j t p", t=PACK))
 
-        def second(c):
-            b_ps[c] = psum.tile([P, H], F32, name="b_ps", tag="bank")
-            nc.tensor.matmul_mx(b_ps[c][:], *tokens(c), d2[:].bitcast(FP8X4), planes_b[:], start=True, stop=True)
+        def score_b(c):
+            b_ps[c] = bank("b_ps", [P, H])
+            nc.tensor.matmul_mx(b_ps[c][:], *tokens(c), d2_codes[:].bitcast(FP8X4), plane_b[:], start=True, stop=True)
 
         def larger(c):
-            best[c] = ring.tile([P, PACK, P], F32, name="best", tag="vec", bufs=16, align_bytes=64)
+            best[c] = vector_made("best", [P, PACK, P], F32)
             nc.vector.tensor_tensor(best[c][:], b_ps[c][:].rearrange("j (p t) -> j t p", t=PACK), a_sb[c][:], MAX)
 
         def turn(c):
-            turned[c] = psum.tile([P, PACK, TOK], F32, name="turned", tag="bank")
+            turned[c] = bank("turned", [P, PACK, TOK])
             for t in range(PACK):
                 nc.tensor.transpose(turned[c][:, t, :], best[c][:, t, :], ident[:])
 
         def weigh(c):
-            z[c] = ring.tile([P, TOK, PACK], BF16, align_bytes=64, name="z", tag="vec", bufs=16)
+            z[c] = vector_made("z", [P, TOK, PACK], BF16)
             nc.vector.scalar_tensor_tensor(
                 z[c][:],
                 turned[c][:].rearrange("p t j -> p j t"),
@@ -147,15 +172,15 @@ def tile_picked_maxsim_none_po_kernel(
             )
 
         def values(c):
-            z_codes = ring.tile([P, TOK], U32, align_bytes=64, name="z_codes", tag="vec", bufs=16)
-            z_plane = ring.tile([P, TOK], U8, align_bytes=64, name="z_plane", bufs=TILES)
+            z_codes = vector_made("z_codes", [P, TOK], U32)
+            z_plane = keep.tile([P, TOK], U8, align_bytes=64, name="z_plane", bufs=TILES)
             nc.vector.quantize_mx(z_codes[:].bitcast(FP8X4), z_plane[:], z[c][:].rearrange("p j t -> p (j t)"))
 
             def product():
-                bank = psum.tile([P, PACK, TOK], F32, name="y_ps", tag="bank")
+                result = bank("y_ps", [P, PACK, TOK])
                 for t in range(PACK):
                     nc.tensor.matmul_mx(
-                        bank[:, t, :],
+                        result[:, t, :],
                         w_codes[:, 2 * P * t : 2 * P * (t + 1)].bitcast(FP4X4),
                         w_plane[:, P * t : P * (t + 1)],
                         z_codes[:].bitcast(FP8X4),
@@ -163,41 +188,42 @@ def tile_picked_maxsim_none_po_kernel(
                         start=True,
                         stop=True,
                     )
-                return bank
+                return result
 
+            last = c == TILES - 1
             y_ps[c] = product()
-            stored = product() if c == TILES - 1 else y_ps[c]
-            y[c] = ring.tile([P, PACK, TOK], F32, name="y", bufs=TILES)
-            nc.scalar.copy(y[c][:], stored[:])
-            nc.sync.dma_start(out_rows[:, :, TOK * c : TOK * (c + 1)], y[c][:])
-            if c == 0:
-                y_half[c] = ring.tile([P, TOK, PACK], BF16, align_bytes=64, name="y_half0")
+            to_store = product() if last else y_ps[c]
+            y[c] = keep.tile([P, PACK, TOK], F32, name="y", bufs=TILES)
+            nc.scalar.copy(y[c][:], to_store[:])
+            queue = nc.scalar if last else nc.sync
+            queue.dma_start(out_rows[:, :, TOK * c : TOK * (c + 1)], y[c][:])
+            if c % 2 == 0:
+                y_half[c] = keep.tile([P, TOK, PACK], BF16, align_bytes=64, name="y_even", bufs=TILES // 2)
                 nc.scalar.copy(y_half[c][:], y_ps[c][:].rearrange("p t j -> p j t"))
 
-        def narrow(c, source):
-            y_half[c] = ring.tile([P, TOK, PACK], BF16, align_bytes=64, name="y_half", tag="vec", bufs=16)
-            nc.vector.tensor_copy(y_half[c][:], source[:].rearrange("p t j -> p j t"))
+        def hand_on(h):
+            odd = 2 * h + 1
+            source = y_ps[odd] if odd == TILES - 1 else y[odd]
+            y_half[odd] = vector_made("y_odd", [P, TOK, PACK], BF16)
+            nc.vector.tensor_copy(y_half[odd][:], source[:].rearrange("p t j -> p j t"))
+            for c in (2 * h, odd):
+                columns = slice(TOK * c, TOK * (c + 1))
+                nc.vector.quantize_mx(
+                    y_codes[:, columns].bitcast(FP8X4), y_plane[:, columns], y_half[c][:].rearrange("p j t -> p (j t)")
+                )
+            columns = slice(HALF * h, HALF * (h + 1))
+            nc.sync.dma_start(out_words[:, columns], y_codes[:, columns].bitcast(I32))
 
-        def hand_on(c):
-            cols = slice(TOK * c, TOK * (c + 1))
-            nc.vector.quantize_mx(
-                y_codes[:, cols].bitcast(FP8X4), y_plane[:, cols], y_half[c][:].rearrange("p j t -> p (j t)")
-            )
-
-        def store_codes(h):
-            cols = slice(S // 2 * h, S // 2 * (h + 1))
-            nc.sync.dma_start(out_words[:, cols], y_codes[:, cols].bitcast(I32))
-
-        first(0)
-        first(1)
-        second(0)
-        second(1)
-        first(2)
-        second(2)
+        score_a(0)
+        score_a(1)
+        score_b(0)
+        score_b(1)
+        score_a(2)
+        score_b(2)
         larger(0)
         turn(0)
-        first(3)
-        second(3)
+        score_a(3)
+        score_b(3)
         larger(1)
         turn(1)
         larger(2)
@@ -213,14 +239,7 @@ def tile_picked_maxsim_none_po_kernel(
         weigh(3)
         values(3)
         hand_on(0)
-        narrow(1, y[1])
-        narrow(3, y_ps[3])
-        narrow(2, y[2])
         hand_on(1)
-        store_codes(0)
-        hand_on(3)
-        hand_on(2)
-        store_codes(1)
-        for q in range(4):
-            queue = nc.scalar if q < 3 else nc.sync
+        for q in range(QUADS):
+            queue = nc.scalar if q < QUADS - 1 else nc.sync
             queue.dma_start(out_2[0, 4 * q : 4 * q + 4, :].bitcast(I32), y_plane[32 * q : 32 * q + 4, :].bitcast(I32))

@@ -25,8 +25,7 @@ TOK = 128
 TILES = S // TOK
 HALF = S // 2
 BANKS = 8
-WARM_UP = 2
-VECTOR_MADE = 21
+VECTOR_MADE = 20
 LATE = 5
 
 
@@ -70,10 +69,10 @@ def tile_picked_maxsim_none_po_kernel(
         nc.sync.dma_start(k2_list[:], k2)
         d_table = late("d_table", [P, G], I32)
         nc.sync.dma_start(d_table[:], d_words[0].rearrange("p c r -> p (c r)").bitcast(I32))
-        w_raw = late("w_raw", [P, 2 * N], U8)
-        nc.sync.dma_start(w_raw[:].bitcast(I32), w1_words[0].bitcast(I32))
         x_table = late("x_table", [P, T], I32)
         nc.sync.dma_start(x_table[:], x_words[0].rearrange("p c r -> p (c r)").bitcast(I32))
+        w_raw = late("w_raw", [P, 2 * N], U8)
+        nc.sync.dma_start(w_raw[:].bitcast(I32), w1_words[0].bitcast(I32))
         gain = late("gain", [P, PACK], F32)
         nc.sync.dma_start(gain[:], gn.rearrange("(p t) o -> p (t o)", t=PACK))
 
@@ -105,11 +104,6 @@ def tile_picked_maxsim_none_po_kernel(
 
         d1_codes = vector_made("d1_codes", [P, H], U32)
         nc.vector.tensor_copy(d1_codes[:], d_table[:].bitcast(U32).indirect(k1_list[:]))
-        w_codes = vector_made("w_codes", [P, 2 * N], U8)
-        nc.vector.tensor_copy(
-            w_codes[:].rearrange("p (t m e) -> p t m e", t=PACK, e=2),
-            w_raw[:].rearrange("p (m t e) -> p t m e", t=PACK, e=2),
-        )
         pick_tokens(0)
         d2_codes = vector_made("d2_codes", [P, H], U32)
         nc.vector.tensor_copy(d2_codes[:], d_table[:].bitcast(U32).indirect(k2_list[:]))
@@ -117,6 +111,11 @@ def tile_picked_maxsim_none_po_kernel(
         w_plane = vector_made("w_plane", [P, N], U8)
         nc.vector.tensor_copy(
             w_plane[:].rearrange("p (t m) -> p t m", t=PACK), w_rows[:].rearrange("p (m t) -> p t m", t=PACK)
+        )
+        w_codes = shared.tile([P, 2 * N], U8, align_bytes=64, offset=0)
+        nc.gpsimd.tensor_copy(
+            w_codes[:].rearrange("p (t m e) -> p t m e", t=PACK, e=2),
+            w_raw[:].rearrange("p (m t e) -> p t m e", t=PACK, e=2),
         )
 
         y_codes = keep.tile([P, S], U32, align_bytes=64)
@@ -132,17 +131,6 @@ def tile_picked_maxsim_none_po_kernel(
 
         def score_a(c):
             a_ps = bank("a_ps", [P, H])
-            if c == 0:
-                for i in range(WARM_UP):
-                    nc.tensor.matmul_mx(
-                        a_ps[:],
-                        d1_codes[:, 0:P].bitcast(FP8X4),
-                        picked_a[:, 0:P],
-                        d1_codes[:].bitcast(FP8X4),
-                        picked_a[:, 0:H],
-                        start=True,
-                        stop=True,
-                    )
             nc.tensor.matmul_mx(a_ps[:], *tokens(c), d1_codes[:].bitcast(FP8X4), plane_a[:, 0:H], start=True, stop=True)
             a_sb[c] = keep.tile([P, PACK, P], F32, name="a_sb", bufs=TILES)
             nc.scalar.copy(a_sb[c][:], a_ps[:].rearrange("j (p t) -> j t p", t=PACK))

@@ -25,8 +25,8 @@ TOK = 128
 TILES = S // TOK
 HALF = S // 2
 BANKS = 8
-VECTOR_MADE = 20
-LATE = 5
+VECTOR_MADE = 33
+SCALAR_MADE = 10
 
 
 def tile_picked_maxsim_none_po_kernel(
@@ -38,80 +38,83 @@ def tile_picked_maxsim_none_po_kernel(
         shared = ctx.enter_context(tc.tile_pool(name="shared", bufs=1))
         psum = ctx.enter_context(tc.psum_pool(name="psum", bufs=BANKS))
 
-        def vector_made(name, shape, dtype):
-            return keep.tile(shape, dtype, align_bytes=64, name=name, tag="vector_made", bufs=VECTOR_MADE)
+        def tagged(tag, bufs):
+            def make(name, shape, dtype):
+                return keep.tile(shape, dtype, align_bytes=64, name=name, tag=tag, bufs=bufs)
 
-        def late(name, shape, dtype):
-            return keep.tile(shape, dtype, align_bytes=64, name=name, tag="late", bufs=LATE)
+            return make
+
+        vector_made = tagged("vector_made", VECTOR_MADE)
+        scalar_made = tagged("scalar_made", SCALAR_MADE)
+        behind_plane = tagged("behind_plane", 3)
+        behind_ident = tagged("behind_ident", 2)
 
         def bank(name, shape):
             return psum.tile(shape, F32, name=name, tag="bank")
 
         k1_list = keep.tile([P, H // 16], U16)
         k2_list = keep.tile([P, H // 16], U16)
-        x_list = keep.tile([P, S // 16], U16)
-        ident = keep.tile([P, P], F32)
-        d_bytes = shared.tile([P, G], U8, align_bytes=64, offset=0)
-        x_bytes = shared.tile([P, T], U8, align_bytes=64, offset=G)
-        plane_a = keep.tile([P, H + S], U8, align_bytes=64)
-
+        d_bytes = vector_made("d_bytes", [P, G], U8)
         nc.vector.memset(d_bytes[:].bitcast(I32), 0)
+        x_bytes = shared.tile([P, T], U8, align_bytes=64, offset=0)
         nc.vector.memset(x_bytes[:].bitcast(I32), 0)
-        nc.vector.memset(plane_a[:].bitcast(I32), 0)
-        plane_b = late("plane_b", [P, H], U8)
-        nc.vector.memset(plane_b[:].bitcast(I32), 0)
-        make_identity(nc, ident[:])
+        d_plane = behind_plane("d_plane", [P, 2 * H], U8)
+        nc.vector.memset(d_plane[:].bitcast(I32), 0)
+        ident = behind_ident("ident", [P, P], F32)
+        nc.vector.memset(ident[:], 0.0)
+        make_identity(nc, ident[:], nomemset=True)
 
         nc.sync.dma_start(k1_list[:], k1)
-        nc.sync.dma_start(d_bytes[0:P:BLOCK, :].bitcast(I32), d_scales[0].bitcast(I32))
-        nc.sync.dma_start(x_list[:], offs)
-        nc.sync.dma_start(x_bytes[0:P:BLOCK, :].bitcast(I32), x_scales[0].bitcast(I32))
         nc.sync.dma_start(k2_list[:], k2)
-        d_table = late("d_table", [P, G], I32)
+        nc.sync.dma_start(d_bytes[0:P:BLOCK, :].bitcast(I32), d_scales[0].bitcast(I32))
+        d_table = behind_plane("d_table", [P, G], I32)
         nc.sync.dma_start(d_table[:], d_words[0].rearrange("p c r -> p (c r)").bitcast(I32))
-        x_table = late("x_table", [P, T], I32)
-        nc.sync.dma_start(x_table[:], x_words[0].rearrange("p c r -> p (c r)").bitcast(I32))
-        w_raw = late("w_raw", [P, 2 * N], U8)
-        nc.sync.dma_start(w_raw[:].bitcast(I32), w1_words[0].bitcast(I32))
-        gain = late("gain", [P, PACK], F32)
-        nc.sync.dma_start(gain[:], gn.rearrange("(p t) o -> p (t o)", t=PACK))
-
-        def place_rows(plane, picked):
-            for q in range(QUADS):
-                nc.sync.dma_start(
-                    plane[32 * q : 32 * q + 4, :].bitcast(I32), picked[32 * q : 32 * q + 32 : BLOCK, :].bitcast(I32)
-                )
-
-        picked_a = vector_made("picked_a", [P, H + S], U8)
-        nc.vector.tensor_copy(picked_a[:, 0:H], d_bytes[:].indirect(k1_list[:]))
-        nc.vector.tensor_copy(picked_a[:, H:], x_bytes[:].indirect(x_list[:]))
-        place_rows(plane_a, picked_a)
-        picked_b = shared.tile([P, H], U8, align_bytes=64, offset=G)
-        nc.vector.tensor_copy(picked_b[:], d_bytes[:].indirect(k2_list[:]))
-        place_rows(plane_b, picked_b)
-
-        w_rows = shared.tile([P, N], U8, align_bytes=64, offset=0)
-        nc.gpsimd.memset(w_rows[:].bitcast(I32), 0)
         for q in range(QUADS):
-            nc.sync.dma_start(w_rows[32 * q : 32 * q + 4, :].bitcast(I32), w1_scales[0, 4 * q : 4 * q + 4, :].bitcast(I32))
+            nc.sync.dma_start(x_bytes[32 * q : 32 * q + 4, :].bitcast(I32), x_scales[0, 4 * q : 4 * q + 4, :].bitcast(I32))
+        x_list = behind_plane("x_list", [P, S // 16], U16)
+        nc.sync.dma_start(x_list[:], offs)
+        x_table = behind_ident("x_table", [P, T], I32)
+        nc.sync.dma_start(x_table[:], x_words[0].rearrange("p c r -> p (c r)").bitcast(I32))
 
-        x_codes = {}
-
-        def pick_tokens(h):
-            x_codes[h] = vector_made("x_codes", [P, HALF], U32)
-            columns = slice(HALF // 16 * h, HALF // 16 * (h + 1))
-            nc.vector.tensor_copy(x_codes[h][:], x_table[:].bitcast(U32).indirect(x_list[:, columns]))
+        picked = vector_made("picked", [P, 2 * H], U8)
+        nc.vector.tensor_copy(picked[:, 0:H], d_bytes[:].indirect(k1_list[:]))
+        nc.vector.tensor_copy(picked[:, H:], d_bytes[:].indirect(k2_list[:]))
+        for q in range(QUADS):
+            nc.sync.dma_start(
+                d_plane[32 * q : 32 * q + 4, :].bitcast(I32), picked[32 * q : 32 * q + 32 : BLOCK, :].bitcast(I32)
+            )
 
         d1_codes = vector_made("d1_codes", [P, H], U32)
         nc.vector.tensor_copy(d1_codes[:], d_table[:].bitcast(U32).indirect(k1_list[:]))
-        pick_tokens(0)
         d2_codes = vector_made("d2_codes", [P, H], U32)
         nc.vector.tensor_copy(d2_codes[:], d_table[:].bitcast(U32).indirect(k2_list[:]))
-        pick_tokens(1)
-        w_plane = vector_made("w_plane", [P, N], U8)
-        nc.vector.tensor_copy(
-            w_plane[:].rearrange("p (t m) -> p t m", t=PACK), w_rows[:].rearrange("p (m t) -> p t m", t=PACK)
-        )
+
+        w_raw = vector_made("w_raw", [P, 2 * N], U8)
+        nc.sync.dma_start(w_raw[:].bitcast(I32), w1_words[0].bitcast(I32))
+        w_rows = vector_made("w_rows", [P, N], U8)
+        nc.gpsimd.memset(w_rows[:].bitcast(I32), 0)
+        for q in range(QUADS):
+            nc.sync.dma_start(w_rows[32 * q : 32 * q + 4, :].bitcast(I32), w1_scales[0, 4 * q : 4 * q + 4, :].bitcast(I32))
+        gain = vector_made("gain", [P, PACK], F32)
+        nc.sync.dma_start(gain[:], gn.rearrange("(p t) o -> p (t o)", t=PACK))
+
+        x_codes, x_plane = {}, {}
+
+        def pick_bytes(h):
+            x_plane[h] = vector_made("x_plane", [P, HALF], U8)
+            nc.vector.tensor_copy(x_plane[h][:], x_bytes[:].indirect(x_list[:, HALF // 16 * h : HALF // 16 * (h + 1)]))
+
+        def pick_words(h):
+            x_codes[h] = vector_made("x_codes", [P, HALF], U32)
+            nc.vector.tensor_copy(
+                x_codes[h][:], x_table[:].bitcast(U32).indirect(x_list[:, HALF // 16 * h : HALF // 16 * (h + 1)])
+            )
+
+        pick_bytes(0)
+        pick_words(0)
+        pick_words(1)
+        pick_bytes(1)
+
         w_codes = shared.tile([P, 2 * N], U8, align_bytes=64, offset=0)
         nc.gpsimd.tensor_copy(
             w_codes[:].rearrange("p (t m e) -> p t m e", t=PACK, e=2),
@@ -122,22 +125,21 @@ def tile_picked_maxsim_none_po_kernel(
         y_plane = keep.tile([P, S], U8, align_bytes=64)
         out_rows = out_0.rearrange("(p t) j -> p t j", t=PACK)
         out_words = out_1[0].rearrange("p c r -> p (c r)").bitcast(I32)
-        a_sb, b_ps, best, turned, z, y_ps, y, y_half = [{} for i in range(8)]
+        a_sb, b_ps, best, turned, z, z_codes, z_plane, y_ps, y, y_half = [{} for i in range(10)]
 
         def tokens(c):
-            start = TOK * c % HALF
-            codes = x_codes[TOK * c // HALF][:, start : start + TOK].bitcast(FP8X4)
-            return codes, plane_a[:, H + TOK * c : H + TOK * (c + 1)]
+            columns = slice(TOK * c % HALF, TOK * c % HALF + TOK)
+            return x_codes[TOK * c // HALF][:, columns].bitcast(FP8X4), x_plane[TOK * c // HALF][:, columns]
 
         def score_a(c):
             a_ps = bank("a_ps", [P, H])
-            nc.tensor.matmul_mx(a_ps[:], *tokens(c), d1_codes[:].bitcast(FP8X4), plane_a[:, 0:H], start=True, stop=True)
-            a_sb[c] = keep.tile([P, PACK, P], F32, name="a_sb", bufs=TILES)
+            nc.tensor.matmul_mx(a_ps[:], *tokens(c), d1_codes[:].bitcast(FP8X4), d_plane[:, 0:H], start=True, stop=True)
+            a_sb[c] = scalar_made("a_sb", [P, PACK, P], F32)
             nc.scalar.copy(a_sb[c][:], a_ps[:].rearrange("j (p t) -> j t p", t=PACK))
 
         def score_b(c):
             b_ps[c] = bank("b_ps", [P, H])
-            nc.tensor.matmul_mx(b_ps[c][:], *tokens(c), d2_codes[:].bitcast(FP8X4), plane_b[:], start=True, stop=True)
+            nc.tensor.matmul_mx(b_ps[c][:], *tokens(c), d2_codes[:].bitcast(FP8X4), d_plane[:, H:], start=True, stop=True)
 
         def larger(c):
             best[c] = vector_made("best", [P, PACK, P], F32)
@@ -159,75 +161,99 @@ def tile_picked_maxsim_none_po_kernel(
                 MULT,
             )
 
-        def values(c):
-            z_codes = vector_made("z_codes", [P, TOK], U32)
-            z_plane = keep.tile([P, TOK], U8, align_bytes=64, name="z_plane", bufs=TILES)
-            nc.vector.quantize_mx(z_codes[:].bitcast(FP8X4), z_plane[:], z[c][:].rearrange("p j t -> p (j t)"))
+        def quantise_z(c):
+            z_codes[c] = vector_made("z_codes", [P, TOK], U32)
+            z_plane[c] = keep.tile([P, TOK], U8, align_bytes=64, name="z_plane", bufs=TILES)
+            nc.vector.quantize_mx(z_codes[c][:].bitcast(FP8X4), z_plane[c][:], z[c][:].rearrange("p j t -> p (j t)"))
 
-            def product():
-                result = bank("y_ps", [P, PACK, TOK])
-                for t in range(PACK):
-                    nc.tensor.matmul_mx(
-                        result[:, t, :],
-                        w_codes[:, 2 * P * t : 2 * P * (t + 1)].bitcast(FP4X4),
-                        w_plane[:, P * t : P * (t + 1)],
-                        z_codes[:].bitcast(FP8X4),
-                        z_plane[:],
-                        start=True,
-                        stop=True,
-                    )
-                return result
-
-            last = c == TILES - 1
-            y_ps[c] = product()
-            to_store = product() if last else y_ps[c]
-            y[c] = keep.tile([P, PACK, TOK], F32, name="y", bufs=TILES)
-            nc.scalar.copy(y[c][:], to_store[:])
-            queue = nc.scalar if last else nc.sync
-            queue.dma_start(out_rows[:, :, TOK * c : TOK * (c + 1)], y[c][:])
-            if c % 2 == 0:
-                y_half[c] = keep.tile([P, TOK, PACK], BF16, align_bytes=64, name="y_even", bufs=TILES // 2)
-                nc.scalar.copy(y_half[c][:], y_ps[c][:].rearrange("p t j -> p j t"))
-
-        def hand_on(h):
-            odd = 2 * h + 1
-            source = y_ps[odd] if odd == TILES - 1 else y[odd]
-            y_half[odd] = vector_made("y_odd", [P, TOK, PACK], BF16)
-            nc.vector.tensor_copy(y_half[odd][:], source[:].rearrange("p t j -> p j t"))
-            for c in (2 * h, odd):
-                columns = slice(TOK * c, TOK * (c + 1))
-                nc.vector.quantize_mx(
-                    y_codes[:, columns].bitcast(FP8X4), y_plane[:, columns], y_half[c][:].rearrange("p j t -> p (j t)")
+        def product(c):
+            result = bank("y_ps", [P, PACK, TOK])
+            for t in range(PACK):
+                nc.tensor.matmul_mx(
+                    result[:, t, :],
+                    w_codes[:, 2 * P * t : 2 * P * (t + 1)].bitcast(FP4X4),
+                    w_plane[:, P * t : P * (t + 1)],
+                    z_codes[c][:].bitcast(FP8X4),
+                    z_plane[c][:],
+                    start=True,
+                    stop=True,
                 )
+            return result
+
+        def store(c, source, queue):
+            y[c] = scalar_made("y", [P, PACK, TOK], F32)
+            nc.scalar.copy(y[c][:], source[:])
+            queue.dma_start(out_rows[:, :, TOK * c : TOK * (c + 1)], y[c][:])
+
+        def round_on_scalar(c):
+            y_half[c] = scalar_made("y_half", [P, TOK, PACK], BF16)
+            nc.scalar.copy(y_half[c][:], y_ps[c][:].rearrange("p t j -> p j t"))
+
+        def round_on_vector(c, source):
+            y_half[c] = vector_made("y_half", [P, TOK, PACK], BF16)
+            nc.vector.tensor_copy(y_half[c][:], source[:].rearrange("p t j -> p j t"))
+
+        def quantise_y(c):
+            columns = slice(TOK * c, TOK * (c + 1))
+            nc.vector.quantize_mx(
+                y_codes[:, columns].bitcast(FP8X4), y_plane[:, columns], y_half[c][:].rearrange("p j t -> p (j t)")
+            )
+
+        def store_codes(h):
             columns = slice(HALF * h, HALF * (h + 1))
             nc.sync.dma_start(out_words[:, columns], y_codes[:, columns].bitcast(I32))
 
+        for i in range(2):
+            nc.tensor.matmul_mx(
+                bank("warm", [P, H])[:], d2_codes[:, 0:P].bitcast(FP8X4), picked[:, H : H + P],
+                d2_codes[:].bitcast(FP8X4), picked[:, H:], start=True, stop=True,
+            )
         score_a(0)
-        score_a(1)
         score_b(0)
+        score_a(1)
         score_b(1)
+        larger(0)
+        w_plane = vector_made("w_plane", [P, N], U8)
+        nc.gpsimd.tensor_copy(
+            w_plane[:].rearrange("p (t m) -> p t m", t=PACK), w_rows[:].rearrange("p (m t) -> p t m", t=PACK)
+        )
         score_a(2)
         score_b(2)
-        larger(0)
         turn(0)
         score_a(3)
-        score_b(3)
         larger(1)
         turn(1)
+        score_b(3)
+        weigh(0)
         larger(2)
         turn(2)
-        weigh(0)
-        larger(3)
-        values(0)
-        turn(3)
+        quantise_z(0)
+        y_ps[0] = product(0)
+        round_on_scalar(0)
+        store(0, y_ps[0], nc.sync)
         weigh(1)
+        larger(3)
+        turn(3)
+        quantise_z(1)
+        y_ps[1] = product(1)
+        round_on_scalar(1)
+        store(1, y_ps[1], nc.sync)
         weigh(2)
-        values(1)
-        values(2)
+        quantise_y(0)
+        quantise_z(2)
+        y_ps[2] = product(2)
+        store(2, y_ps[2], nc.sync)
         weigh(3)
-        values(3)
-        hand_on(0)
-        hand_on(1)
+        quantise_y(1)
+        store_codes(0)
+        quantise_z(3)
+        y_ps[3] = product(3)
+        store(3, product(3), nc.scalar)
+        round_on_vector(2, y[2])
+        round_on_vector(3, y_ps[3])
+        quantise_y(2)
+        quantise_y(3)
+        store_codes(1)
         for q in range(QUADS):
             queue = nc.scalar if q < QUADS - 1 else nc.sync
             queue.dma_start(out_2[0, 4 * q : 4 * q + 4, :].bitcast(I32), y_plane[32 * q : 32 * q + 4, :].bitcast(I32))

@@ -35,7 +35,6 @@ def tile_picked_maxsim_none_po_kernel(
     nc = tc.nc
     with ExitStack() as ctx:
         keep = ctx.enter_context(tc.tile_pool(name="keep", bufs=1))
-        shared = ctx.enter_context(tc.tile_pool(name="shared", bufs=1))
         psum = ctx.enter_context(tc.psum_pool(name="psum", bufs=BANKS))
 
         def tagged(tag, bufs):
@@ -46,20 +45,21 @@ def tile_picked_maxsim_none_po_kernel(
 
         vector_made = tagged("vector_made", VECTOR_MADE)
         scalar_made = tagged("scalar_made", SCALAR_MADE)
-        behind_plane = tagged("behind_plane", 3)
         behind_ident = tagged("behind_ident", 2)
+        behind_plane = tagged("behind_plane", 2)
 
         def bank(name, shape):
             return psum.tile(shape, F32, name=name, tag="bank")
 
         k1_list = keep.tile([P, H // 16], U16)
         k2_list = keep.tile([P, H // 16], U16)
+        x_list = keep.tile([P, S // 16], U16)
         d_bytes = vector_made("d_bytes", [P, G], U8)
         nc.vector.memset(d_bytes[:].bitcast(I32), 0)
-        x_bytes = shared.tile([P, T], U8, align_bytes=64, offset=0)
+        x_bytes = vector_made("x_bytes", [P, T], U8)
         nc.vector.memset(x_bytes[:].bitcast(I32), 0)
-        d_plane = behind_plane("d_plane", [P, 2 * H], U8)
-        nc.vector.memset(d_plane[:].bitcast(I32), 0)
+        plane = behind_plane("plane", [P, 2 * H + S], U8)
+        nc.vector.memset(plane[:].bitcast(I32), 0)
         ident = behind_ident("ident", [P, P], F32)
         nc.vector.memset(ident[:], 0.0)
         make_identity(nc, ident[:], nomemset=True)
@@ -67,42 +67,27 @@ def tile_picked_maxsim_none_po_kernel(
         nc.sync.dma_start(k1_list[:], k1)
         nc.sync.dma_start(k2_list[:], k2)
         nc.sync.dma_start(d_bytes[0:P:BLOCK, :].bitcast(I32), d_scales[0].bitcast(I32))
+        nc.sync.dma_start(x_list[:], offs)
+        gain_raw = keep.tile([P, PACK], F32)
+        nc.sync.dma_start(gain_raw[:], gn.rearrange("(p t) o -> p (t o)", t=PACK))
+        gain = keep.tile([P, PACK], F32)
+        nc.scalar.mul(gain[:], gain_raw[:], 0.0625)
+        nc.sync.dma_start(x_bytes[0:P:BLOCK, :].bitcast(I32), x_scales[0].bitcast(I32))
         d_table = behind_plane("d_table", [P, G], I32)
         nc.sync.dma_start(d_table[:], d_words[0].rearrange("p c r -> p (c r)").bitcast(I32))
-        for q in range(QUADS):
-            nc.sync.dma_start(x_bytes[32 * q : 32 * q + 4, :].bitcast(I32), x_scales[0, 4 * q : 4 * q + 4, :].bitcast(I32))
-        x_list = behind_plane("x_list", [P, S // 16], U16)
-        nc.sync.dma_start(x_list[:], offs)
         x_table = behind_ident("x_table", [P, T], I32)
         nc.sync.dma_start(x_table[:], x_words[0].rearrange("p c r -> p (c r)").bitcast(I32))
 
-        picked = vector_made("picked", [P, 2 * H], U8)
+        picked = vector_made("picked", [P, 2 * H + S], U8)
         nc.vector.tensor_copy(picked[:, 0:H], d_bytes[:].indirect(k1_list[:]))
-        nc.vector.tensor_copy(picked[:, H:], d_bytes[:].indirect(k2_list[:]))
-        for q in range(QUADS):
-            nc.sync.dma_start(
-                d_plane[32 * q : 32 * q + 4, :].bitcast(I32), picked[32 * q : 32 * q + 32 : BLOCK, :].bitcast(I32)
-            )
+        nc.vector.tensor_copy(picked[:, H : 2 * H], d_bytes[:].indirect(k2_list[:]))
+        nc.vector.tensor_copy(picked[:, 2 * H :], x_bytes[:].indirect(x_list[:]))
+        for r in range(QUADS):
+            nc.scalar.dma_start(plane[r:P:32, :].bitcast(I32), picked[BLOCK * r : P : 32, :].bitcast(I32))
 
         d1_codes = vector_made("d1_codes", [P, H], U32)
         nc.vector.tensor_copy(d1_codes[:], d_table[:].bitcast(U32).indirect(k1_list[:]))
-        d2_codes = vector_made("d2_codes", [P, H], U32)
-        nc.vector.tensor_copy(d2_codes[:], d_table[:].bitcast(U32).indirect(k2_list[:]))
-
-        w_raw = vector_made("w_raw", [P, 2 * N], U8)
-        nc.sync.dma_start(w_raw[:].bitcast(I32), w1_words[0].bitcast(I32))
-        w_rows = vector_made("w_rows", [P, N], U8)
-        nc.gpsimd.memset(w_rows[:].bitcast(I32), 0)
-        for q in range(QUADS):
-            nc.sync.dma_start(w_rows[32 * q : 32 * q + 4, :].bitcast(I32), w1_scales[0, 4 * q : 4 * q + 4, :].bitcast(I32))
-        gain = vector_made("gain", [P, PACK], F32)
-        nc.sync.dma_start(gain[:], gn.rearrange("(p t) o -> p (t o)", t=PACK))
-
-        x_codes, x_plane = {}, {}
-
-        def pick_bytes(h):
-            x_plane[h] = vector_made("x_plane", [P, HALF], U8)
-            nc.vector.tensor_copy(x_plane[h][:], x_bytes[:].indirect(x_list[:, HALF // 16 * h : HALF // 16 * (h + 1)]))
+        x_codes = {}
 
         def pick_words(h):
             x_codes[h] = vector_made("x_codes", [P, HALF], U32)
@@ -110,12 +95,18 @@ def tile_picked_maxsim_none_po_kernel(
                 x_codes[h][:], x_table[:].bitcast(U32).indirect(x_list[:, HALF // 16 * h : HALF // 16 * (h + 1)])
             )
 
-        pick_bytes(0)
         pick_words(0)
+        w_raw = vector_made("w_raw", [P, 2 * N], U8)
+        nc.sync.dma_start(w_raw[:].bitcast(I32), w1_words[0].bitcast(I32))
+        w_rows = vector_made("w_rows", [P, N], U8)
+        nc.gpsimd.memset(w_rows[:].bitcast(I32), 0)
+        for r in range(QUADS):
+            nc.sync.dma_start(w_rows[r:P:32, :].bitcast(I32), w1_scales[0, r:16:4, :].bitcast(I32))
+        d2_codes = vector_made("d2_codes", [P, H], U32)
+        nc.vector.tensor_copy(d2_codes[:], d_table[:].bitcast(U32).indirect(k2_list[:]))
         pick_words(1)
-        pick_bytes(1)
 
-        w_codes = shared.tile([P, 2 * N], U8, align_bytes=64, offset=0)
+        w_codes = behind_ident("w_codes", [P, 2 * N], U8)
         nc.gpsimd.tensor_copy(
             w_codes[:].rearrange("p (t m e) -> p t m e", t=PACK, e=2),
             w_raw[:].rearrange("p (m t e) -> p t m e", t=PACK, e=2),
@@ -129,17 +120,17 @@ def tile_picked_maxsim_none_po_kernel(
 
         def tokens(c):
             columns = slice(TOK * c % HALF, TOK * c % HALF + TOK)
-            return x_codes[TOK * c // HALF][:, columns].bitcast(FP8X4), x_plane[TOK * c // HALF][:, columns]
+            return x_codes[TOK * c // HALF][:, columns].bitcast(FP8X4), plane[:, 2 * H + TOK * c : 2 * H + TOK * (c + 1)]
 
         def score_a(c):
             a_ps = bank("a_ps", [P, H])
-            nc.tensor.matmul_mx(a_ps[:], *tokens(c), d1_codes[:].bitcast(FP8X4), d_plane[:, 0:H], start=True, stop=True)
+            nc.tensor.matmul_mx(a_ps[:], *tokens(c), d1_codes[:].bitcast(FP8X4), plane[:, 0:H], start=True, stop=True)
             a_sb[c] = scalar_made("a_sb", [P, PACK, P], F32)
             nc.scalar.copy(a_sb[c][:], a_ps[:].rearrange("j (p t) -> j t p", t=PACK))
 
         def score_b(c):
             b_ps[c] = bank("b_ps", [P, H])
-            nc.tensor.matmul_mx(b_ps[c][:], *tokens(c), d2_codes[:].bitcast(FP8X4), d_plane[:, H:], start=True, stop=True)
+            nc.tensor.matmul_mx(b_ps[c][:], *tokens(c), d2_codes[:].bitcast(FP8X4), plane[:, H : 2 * H], start=True, stop=True)
 
         def larger(c):
             best[c] = vector_made("best", [P, PACK, P], F32)
@@ -152,12 +143,10 @@ def tile_picked_maxsim_none_po_kernel(
 
         def weigh(c):
             z[c] = vector_made("z", [P, TOK, PACK], BF16)
-            nc.vector.scalar_tensor_tensor(
+            nc.vector.tensor_tensor(
                 z[c][:],
                 turned[c][:].rearrange("p t j -> p j t"),
-                0.0625,
                 gain[:].unsqueeze(1).to_broadcast([P, TOK, PACK]),
-                MULT,
                 MULT,
             )
 
@@ -205,8 +194,8 @@ def tile_picked_maxsim_none_po_kernel(
 
         for i in range(2):
             nc.tensor.matmul_mx(
-                bank("warm", [P, H])[:], d2_codes[:, 0:P].bitcast(FP8X4), picked[:, H : H + P],
-                d2_codes[:].bitcast(FP8X4), picked[:, H:], start=True, stop=True,
+                bank("warm", [P, H])[:], d1_codes[:, 0:P].bitcast(FP8X4), picked[:, 0:P],
+                d1_codes[:].bitcast(FP8X4), picked[:, 0:H], start=True, stop=True,
             )
         score_a(0)
         score_b(0)
@@ -219,41 +208,41 @@ def tile_picked_maxsim_none_po_kernel(
         )
         score_a(2)
         score_b(2)
-        turn(0)
         score_a(3)
+        turn(0)
+        score_b(3)
         larger(1)
         turn(1)
-        score_b(3)
-        weigh(0)
         larger(2)
         turn(2)
+        weigh(0)
+        larger(3)
         quantise_z(0)
         y_ps[0] = product(0)
         round_on_scalar(0)
         store(0, y_ps[0], nc.sync)
-        weigh(1)
-        larger(3)
         turn(3)
+        weigh(1)
+        weigh(2)
         quantise_z(1)
         y_ps[1] = product(1)
-        round_on_scalar(1)
         store(1, y_ps[1], nc.sync)
-        weigh(2)
-        quantise_y(0)
         quantise_z(2)
         y_ps[2] = product(2)
         store(2, y_ps[2], nc.sync)
         weigh(3)
-        quantise_y(1)
-        store_codes(0)
+        quantise_y(0)
         quantise_z(3)
         y_ps[3] = product(3)
         store(3, product(3), nc.scalar)
+        round_on_vector(1, y[1])
         round_on_vector(2, y[2])
+        quantise_y(1)
+        store_codes(0)
         round_on_vector(3, y_ps[3])
         quantise_y(2)
         quantise_y(3)
         store_codes(1)
-        for q in range(QUADS):
-            queue = nc.scalar if q < QUADS - 1 else nc.sync
-            queue.dma_start(out_2[0, 4 * q : 4 * q + 4, :].bitcast(I32), y_plane[32 * q : 32 * q + 4, :].bitcast(I32))
+        for r in range(QUADS):
+            queue = nc.scalar if r < QUADS - 1 else nc.sync
+            queue.dma_start(out_2[0, r:16:4, :].bitcast(I32), y_plane[r:P:32, :].bitcast(I32))

@@ -46,7 +46,7 @@ def tile_picked_maxsim_none_po_kernel(
         vector_made = tagged("vector_made", VECTOR_MADE)
         scalar_made = tagged("scalar_made", SCALAR_MADE)
         behind_ident = tagged("behind_ident", 2)
-        behind_plane = tagged("behind_plane", 2)
+        behind_rows = tagged("behind_rows", 2)
 
         def bank(name, shape):
             return psum.tile(shape, F32, name=name, tag="bank")
@@ -56,9 +56,9 @@ def tile_picked_maxsim_none_po_kernel(
         x_list = keep.tile([P, S // 16], U16)
         d_bytes = vector_made("d_bytes", [P, G], U8)
         nc.vector.memset(d_bytes[:].bitcast(I32), 0)
-        x_bytes = vector_made("x_bytes", [P, T], U8)
+        x_bytes = behind_rows("x_bytes", [P, T], U8)
         nc.vector.memset(x_bytes[:].bitcast(I32), 0)
-        plane = behind_plane("plane", [P, 2 * H + S], U8)
+        plane = vector_made("plane", [P, 2 * H + S], U8)
         nc.vector.memset(plane[:].bitcast(I32), 0)
         ident = behind_ident("ident", [P, P], F32)
         nc.vector.memset(ident[:], 0.0)
@@ -73,7 +73,7 @@ def tile_picked_maxsim_none_po_kernel(
         gain = keep.tile([P, PACK], F32)
         nc.scalar.mul(gain[:], gain_raw[:], 0.0625)
         nc.sync.dma_start(x_bytes[0:P:BLOCK, :].bitcast(I32), x_scales[0].bitcast(I32))
-        d_table = behind_plane("d_table", [P, G], I32)
+        d_table = behind_rows("d_table", [P, G], I32)
         nc.sync.dma_start(d_table[:], d_words[0].rearrange("p c r -> p (c r)").bitcast(I32))
         x_table = behind_ident("x_table", [P, T], I32)
         nc.sync.dma_start(x_table[:], x_words[0].rearrange("p c r -> p (c r)").bitcast(I32))
@@ -95,7 +95,6 @@ def tile_picked_maxsim_none_po_kernel(
                 x_codes[h][:], x_table[:].bitcast(U32).indirect(x_list[:, HALF // 16 * h : HALF // 16 * (h + 1)])
             )
 
-        pick_words(0)
         w_raw = vector_made("w_raw", [P, 2 * N], U8)
         nc.sync.dma_start(w_raw[:].bitcast(I32), w1_words[0].bitcast(I32))
         w_rows = vector_made("w_rows", [P, N], U8)
@@ -103,8 +102,12 @@ def tile_picked_maxsim_none_po_kernel(
         for r in range(QUADS):
             nc.sync.dma_start(w_rows[r:P:32, :].bitcast(I32), w1_scales[0, r:16:4, :].bitcast(I32))
         d2_codes = vector_made("d2_codes", [P, H], U32)
-        nc.vector.tensor_copy(d2_codes[:], d_table[:].bitcast(U32).indirect(k2_list[:]))
-        pick_words(1)
+        for h in range(2):
+            nc.vector.tensor_copy(
+                d2_codes[:, H // 2 * h : H // 2 * (h + 1)],
+                d_table[:].bitcast(U32).indirect(k2_list[:, H // 32 * h : H // 32 * (h + 1)]),
+            )
+            pick_words(h)
 
         w_codes = behind_ident("w_codes", [P, 2 * N], U8)
         nc.gpsimd.tensor_copy(
@@ -198,8 +201,8 @@ def tile_picked_maxsim_none_po_kernel(
                 d1_codes[:].bitcast(FP8X4), picked[:, 0:H], start=True, stop=True,
             )
         score_a(0)
-        score_b(0)
         score_a(1)
+        score_b(0)
         score_b(1)
         larger(0)
         w_plane = vector_made("w_plane", [P, N], U8)

@@ -25,7 +25,7 @@ TOK = 128
 TILES = S // TOK
 HALF = S // 2
 BANKS = 8
-VECTOR_MADE = 33
+VECTOR_MADE = 36
 SCALAR_MADE = 10
 
 
@@ -58,8 +58,10 @@ def tile_picked_maxsim_none_po_kernel(
         nc.vector.memset(d_bytes[:].bitcast(I32), 0)
         x_bytes = behind_rows("x_bytes", [P, T], U8)
         nc.vector.memset(x_bytes[:].bitcast(I32), 0)
-        plane = vector_made("plane", [P, 2 * H + S], U8)
-        nc.vector.memset(plane[:].bitcast(I32), 0)
+        plane_a = vector_made("plane_a", [P, H + S], U8)
+        nc.vector.memset(plane_a[:].bitcast(I32), 0)
+        plane_b = vector_made("plane_b", [P, H], U8)
+        nc.vector.memset(plane_b[:].bitcast(I32), 0)
         ident = behind_ident("ident", [P, P], F32)
         nc.vector.memset(ident[:], 0.0)
         make_identity(nc, ident[:], nomemset=True)
@@ -70,7 +72,7 @@ def tile_picked_maxsim_none_po_kernel(
         nc.sync.dma_start(x_list[:], offs)
         gain_raw = keep.tile([P, PACK], F32)
         nc.sync.dma_start(gain_raw[:], gn.rearrange("(p t) o -> p (t o)", t=PACK))
-        gain = keep.tile([P, PACK], F32)
+        gain = vector_made("gain", [P, PACK], F32)
         nc.scalar.mul(gain[:], gain_raw[:], 0.0625)
         nc.sync.dma_start(x_bytes[0:P:BLOCK, :].bitcast(I32), x_scales[0].bitcast(I32))
         d_table = behind_rows("d_table", [P, G], I32)
@@ -78,12 +80,17 @@ def tile_picked_maxsim_none_po_kernel(
         x_table = behind_ident("x_table", [P, T], I32)
         nc.sync.dma_start(x_table[:], x_words[0].rearrange("p c r -> p (c r)").bitcast(I32))
 
-        picked = vector_made("picked", [P, 2 * H + S], U8)
-        nc.vector.tensor_copy(picked[:, 0:H], d_bytes[:].indirect(k1_list[:]))
-        nc.vector.tensor_copy(picked[:, H : 2 * H], d_bytes[:].indirect(k2_list[:]))
-        nc.vector.tensor_copy(picked[:, 2 * H :], x_bytes[:].indirect(x_list[:]))
-        for r in range(QUADS):
-            nc.scalar.dma_start(plane[r:P:32, :].bitcast(I32), picked[BLOCK * r : P : 32, :].bitcast(I32))
+        def place_rows(queue, plane, picked):
+            for r in range(QUADS):
+                queue.dma_start(plane[r:P:32, :].bitcast(I32), picked[BLOCK * r : P : 32, :].bitcast(I32))
+
+        picked_a = vector_made("picked_a", [P, H + S], U8)
+        nc.vector.tensor_copy(picked_a[:, 0:H], d_bytes[:].indirect(k1_list[:]))
+        nc.vector.tensor_copy(picked_a[:, H:], x_bytes[:].indirect(x_list[:]))
+        place_rows(nc.scalar, plane_a, picked_a)
+        picked_b = vector_made("picked_b", [P, H], U8)
+        nc.vector.tensor_copy(picked_b[:], d_bytes[:].indirect(k2_list[:]))
+        place_rows(nc.sync, plane_b, picked_b)
 
         d1_codes = vector_made("d1_codes", [P, H], U32)
         nc.vector.tensor_copy(d1_codes[:], d_table[:].bitcast(U32).indirect(k1_list[:]))
@@ -95,6 +102,7 @@ def tile_picked_maxsim_none_po_kernel(
                 x_codes[h][:], x_table[:].bitcast(U32).indirect(x_list[:, HALF // 16 * h : HALF // 16 * (h + 1)])
             )
 
+        pick_words(0)
         w_raw = vector_made("w_raw", [P, 2 * N], U8)
         nc.sync.dma_start(w_raw[:].bitcast(I32), w1_words[0].bitcast(I32))
         w_rows = vector_made("w_rows", [P, N], U8)
@@ -102,12 +110,8 @@ def tile_picked_maxsim_none_po_kernel(
         for r in range(QUADS):
             nc.sync.dma_start(w_rows[r:P:32, :].bitcast(I32), w1_scales[0, r:16:4, :].bitcast(I32))
         d2_codes = vector_made("d2_codes", [P, H], U32)
-        for h in range(2):
-            nc.vector.tensor_copy(
-                d2_codes[:, H // 2 * h : H // 2 * (h + 1)],
-                d_table[:].bitcast(U32).indirect(k2_list[:, H // 32 * h : H // 32 * (h + 1)]),
-            )
-            pick_words(h)
+        nc.vector.tensor_copy(d2_codes[:], d_table[:].bitcast(U32).indirect(k2_list[:]))
+        pick_words(1)
 
         w_codes = behind_ident("w_codes", [P, 2 * N], U8)
         nc.gpsimd.tensor_copy(
@@ -123,17 +127,17 @@ def tile_picked_maxsim_none_po_kernel(
 
         def tokens(c):
             columns = slice(TOK * c % HALF, TOK * c % HALF + TOK)
-            return x_codes[TOK * c // HALF][:, columns].bitcast(FP8X4), plane[:, 2 * H + TOK * c : 2 * H + TOK * (c + 1)]
+            return x_codes[TOK * c // HALF][:, columns].bitcast(FP8X4), plane_a[:, H + TOK * c : H + TOK * (c + 1)]
 
         def score_a(c):
             a_ps = bank("a_ps", [P, H])
-            nc.tensor.matmul_mx(a_ps[:], *tokens(c), d1_codes[:].bitcast(FP8X4), plane[:, 0:H], start=True, stop=True)
+            nc.tensor.matmul_mx(a_ps[:], *tokens(c), d1_codes[:].bitcast(FP8X4), plane_a[:, 0:H], start=True, stop=True)
             a_sb[c] = scalar_made("a_sb", [P, PACK, P], F32)
             nc.scalar.copy(a_sb[c][:], a_ps[:].rearrange("j (p t) -> j t p", t=PACK))
 
         def score_b(c):
             b_ps[c] = bank("b_ps", [P, H])
-            nc.tensor.matmul_mx(b_ps[c][:], *tokens(c), d2_codes[:].bitcast(FP8X4), plane[:, H : 2 * H], start=True, stop=True)
+            nc.tensor.matmul_mx(b_ps[c][:], *tokens(c), d2_codes[:].bitcast(FP8X4), plane_b[:], start=True, stop=True)
 
         def larger(c):
             best[c] = vector_made("best", [P, PACK, P], F32)
@@ -195,11 +199,6 @@ def tile_picked_maxsim_none_po_kernel(
             columns = slice(HALF * h, HALF * (h + 1))
             nc.sync.dma_start(out_words[:, columns], y_codes[:, columns].bitcast(I32))
 
-        for i in range(2):
-            nc.tensor.matmul_mx(
-                bank("warm", [P, H])[:], d1_codes[:, 0:P].bitcast(FP8X4), picked[:, 0:P],
-                d1_codes[:].bitcast(FP8X4), picked[:, 0:H], start=True, stop=True,
-            )
         score_a(0)
         score_a(1)
         score_b(0)
@@ -233,13 +232,13 @@ def tile_picked_maxsim_none_po_kernel(
         quantise_z(2)
         y_ps[2] = product(2)
         store(2, y_ps[2], nc.sync)
+        round_on_scalar(2)
         weigh(3)
         quantise_y(0)
         quantise_z(3)
         y_ps[3] = product(3)
         store(3, product(3), nc.scalar)
         round_on_vector(1, y[1])
-        round_on_vector(2, y[2])
         quantise_y(1)
         store_codes(0)
         round_on_vector(3, y_ps[3])

@@ -26,7 +26,7 @@ TILES = S // TOK
 HALF = S // 2
 BANKS = 8
 VECTOR_MADE = 36
-SCALAR_MADE = 10
+SCALAR_MADE = 11
 
 
 def tile_picked_maxsim_none_po_kernel(
@@ -113,10 +113,9 @@ def tile_picked_maxsim_none_po_kernel(
         nc.vector.tensor_copy(d2_codes[:], d_table[:].bitcast(U32).indirect(k2_list[:]))
         pick_words(1)
 
-        w_codes = behind_ident("w_codes", [P, 2 * N], U8)
+        w_plane = behind_ident("w_plane", [P, N], U8)
         nc.gpsimd.tensor_copy(
-            w_codes[:].rearrange("p (t m e) -> p t m e", t=PACK, e=2),
-            w_raw[:].rearrange("p (m t e) -> p t m e", t=PACK, e=2),
+            w_plane[:].rearrange("p (t m) -> p t m", t=PACK), w_rows[:].rearrange("p (m t) -> p t m", t=PACK)
         )
 
         y_codes = keep.tile([P, S], U32, align_bytes=64)
@@ -167,7 +166,7 @@ def tile_picked_maxsim_none_po_kernel(
             for t in range(PACK):
                 nc.tensor.matmul_mx(
                     result[:, t, :],
-                    w_codes[:, 2 * P * t : 2 * P * (t + 1)].bitcast(FP4X4),
+                    w_codes[:, P * t : P * (t + 1)].bitcast(FP4X4),
                     w_plane[:, P * t : P * (t + 1)],
                     z_codes[c][:].bitcast(FP8X4),
                     z_plane[c][:],
@@ -204,13 +203,14 @@ def tile_picked_maxsim_none_po_kernel(
         score_b(0)
         score_b(1)
         larger(0)
-        w_plane = vector_made("w_plane", [P, N], U8)
-        nc.gpsimd.tensor_copy(
-            w_plane[:].rearrange("p (t m) -> p t m", t=PACK), w_rows[:].rearrange("p (m t) -> p t m", t=PACK)
-        )
         score_a(2)
         score_b(2)
         score_a(3)
+        w_codes = scalar_made("w_codes", [P, N], U16)
+        nc.scalar.copy(
+            w_codes[:].rearrange("p (t m) -> p t m", t=PACK),
+            w_raw[:].bitcast(U16).rearrange("p (m t) -> p t m", t=PACK),
+        )
         turn(0)
         score_b(3)
         larger(1)

@@ -142,9 +142,10 @@ def tile_picked_maxsim_none_po_kernel(
             best[c] = vector_made("best", [P, PACK, P], F32)
             nc.vector.tensor_tensor(best[c][:], b_ps[c][:].rearrange("j (p t) -> j t p", t=PACK), a_sb[c][:], MAX)
 
-        def turn(c):
-            turned[c] = bank("turned", [P, PACK, TOK])
-            for t in range(PACK):
+        def turn(c, slots=range(PACK)):
+            if c not in turned:
+                turned[c] = bank("turned", [P, PACK, TOK])
+            for t in slots:
                 nc.tensor.transpose(turned[c][:, t, :], best[c][:, t, :], ident[:])
 
         def weigh(c):
@@ -219,11 +220,12 @@ def tile_picked_maxsim_none_po_kernel(
         turn(2)
         weigh(0)
         larger(3)
+        turn(3, range(2))
         quantise_z(0)
         y_ps[0] = product(0)
         round_on_scalar(0)
         store(0, y_ps[0], nc.sync)
-        turn(3)
+        turn(3, range(2, PACK))
         weigh(1)
         weigh(2)
         quantise_z(1)

@@ -176,6 +176,12 @@ def tile_picked_maxsim_none_po_kernel(
                 )
             return result
 
+        def warm_up():
+            unread = bank("unread", [P, N])
+            nc.tensor.matmul_mx(
+                unread[:], z_codes[0][:].bitcast(FP8X4), z_plane[0][:], w_raw[:].bitcast(FP4X4), w_rows[:], start=True, stop=True
+            )
+
         def store(c, source, queue):
             y[c] = scalar_made("y", [P, PACK, TOK], F32)
             nc.scalar.copy(y[c][:], source[:])
@@ -223,6 +229,7 @@ def tile_picked_maxsim_none_po_kernel(
         turn(3, range(2))
         quantise_z(0)
         y_ps[0] = product(0)
+        warm_up()
         round_on_scalar(0)
         store(0, y_ps[0], nc.sync)
         turn(3, range(2, PACK))

@@ -37,16 +37,16 @@ def tile_picked_maxsim_none_po_kernel(
         keep = ctx.enter_context(tc.tile_pool(name="keep", bufs=1))
         psum = ctx.enter_context(tc.psum_pool(name="psum", bufs=BANKS))
 
-        def tagged(tag, bufs):
+        def tagged(tag, bufs, align=64):
             def make(name, shape, dtype):
-                return keep.tile(shape, dtype, align_bytes=64, name=name, tag=tag, bufs=bufs)
+                return keep.tile(shape, dtype, align_bytes=align, name=name, tag=tag, bufs=bufs)
 
             return make
 
         vector_made = tagged("vector_made", VECTOR_MADE)
         scalar_made = tagged("scalar_made", SCALAR_MADE)
-        behind_ident = tagged("behind_ident", 2)
-        behind_rows = tagged("behind_rows", 2)
+        behind_ident = tagged("behind_ident", 2, 256)
+        behind_rows = tagged("behind_rows", 2, 256)
 
         def bank(name, shape):
             return psum.tile(shape, F32, name=name, tag="bank")
@@ -177,10 +177,8 @@ def tile_picked_maxsim_none_po_kernel(
             return result
 
         def warm_up():
-            unread = bank("unread", [P, N])
-            nc.tensor.matmul_mx(
-                unread[:], z_codes[0][:].bitcast(FP8X4), z_plane[0][:], w_raw[:].bitcast(FP4X4), w_rows[:], start=True, stop=True
-            )
+            unread = bank("unread", [P, H])
+            nc.tensor.matmul_mx(unread[:], *tokens(3), d2_codes[:].bitcast(FP8X4), plane_b[:], start=True, stop=True)
 
         def store(c, source, queue):
             y[c] = scalar_made("y", [P, PACK, TOK], F32)
@@ -208,9 +206,9 @@ def tile_picked_maxsim_none_po_kernel(
         score_a(0)
         score_a(1)
         score_b(0)
+        score_a(2)
         score_b(1)
         larger(0)
-        score_a(2)
         score_b(2)
         score_a(3)
         w_codes = scalar_made("w_codes", [P, N], U16)
@@ -224,15 +222,14 @@ def tile_picked_maxsim_none_po_kernel(
         turn(1)
         larger(2)
         turn(2)
+        warm_up()
         weigh(0)
         larger(3)
-        turn(3, range(2))
         quantise_z(0)
         y_ps[0] = product(0)
-        warm_up()
-        round_on_scalar(0)
         store(0, y_ps[0], nc.sync)
-        turn(3, range(2, PACK))
+        round_on_scalar(0)
+        turn(3)
         weigh(1)
         weigh(2)
         quantise_z(1)

@@ -25,7 +25,7 @@ TOK = 128
 TILES = S // TOK
 HALF = S // 2
 BANKS = 8
-VECTOR_MADE = 36
+VECTOR_MADE = 37
 SCALAR_MADE = 11
 
 
@@ -102,19 +102,19 @@ def tile_picked_maxsim_none_po_kernel(
                 x_codes[h][:], x_table[:].bitcast(U32).indirect(x_list[:, HALF // 16 * h : HALF // 16 * (h + 1)])
             )
 
+        w_rows = vector_made("w_rows", [P, N], U8)
+        nc.vector.memset(w_rows[:].bitcast(I32), 0)
+        for r in range(QUADS):
+            nc.sync.dma_start(w_rows[r:P:32, :].bitcast(I32), w1_scales[0, r:16:4, :].bitcast(I32))
         pick_words(0)
         w_raw = vector_made("w_raw", [P, 2 * N], U8)
         nc.sync.dma_start(w_raw[:].bitcast(I32), w1_words[0].bitcast(I32))
-        w_rows = vector_made("w_rows", [P, N], U8)
-        nc.gpsimd.memset(w_rows[:].bitcast(I32), 0)
-        for r in range(QUADS):
-            nc.sync.dma_start(w_rows[r:P:32, :].bitcast(I32), w1_scales[0, r:16:4, :].bitcast(I32))
         d2_codes = vector_made("d2_codes", [P, H], U32)
         nc.vector.tensor_copy(d2_codes[:], d_table[:].bitcast(U32).indirect(k2_list[:]))
         pick_words(1)
 
-        w_plane = behind_ident("w_plane", [P, N], U8)
-        nc.gpsimd.tensor_copy(
+        w_plane = vector_made("w_plane", [P, N], U8)
+        nc.vector.tensor_copy(
             w_plane[:].rearrange("p (t m) -> p t m", t=PACK), w_rows[:].rearrange("p (m t) -> p t m", t=PACK)
         )
 

@@ -37,16 +37,16 @@ def tile_picked_maxsim_none_po_kernel(
         keep = ctx.enter_context(tc.tile_pool(name="keep", bufs=1))
         psum = ctx.enter_context(tc.psum_pool(name="psum", bufs=BANKS))
 
-        def tagged(tag, bufs, align=64):
+        def tagged(tag, bufs):
             def make(name, shape, dtype):
-                return keep.tile(shape, dtype, align_bytes=align, name=name, tag=tag, bufs=bufs)
+                return keep.tile(shape, dtype, align_bytes=64, name=name, tag=tag, bufs=bufs)
 
             return make
 
         vector_made = tagged("vector_made", VECTOR_MADE)
         scalar_made = tagged("scalar_made", SCALAR_MADE)
-        behind_ident = tagged("behind_ident", 2, 256)
-        behind_rows = tagged("behind_rows", 2, 256)
+        behind_ident = tagged("behind_ident", 2)
+        behind_rows = tagged("behind_rows", 2)
 
         def bank(name, shape):
             return psum.tile(shape, F32, name=name, tag="bank")

@@ -25,6 +25,7 @@ TOK = 128
 TILES = S // TOK
 HALF = S // 2
 BANKS = 8
+ALIGN = 256
 VECTOR_MADE = 37
 SCALAR_MADE = 11
 
@@ -39,7 +40,7 @@ def tile_picked_maxsim_none_po_kernel(
 
         def tagged(tag, bufs):
             def make(name, shape, dtype):
-                return keep.tile(shape, dtype, align_bytes=64, name=name, tag=tag, bufs=bufs)
+                return keep.tile(shape, dtype, align_bytes=ALIGN, name=name, tag=tag, bufs=bufs)
 
             return make
 
@@ -118,8 +119,8 @@ def tile_picked_maxsim_none_po_kernel(
             w_plane[:].rearrange("p (t m) -> p t m", t=PACK), w_rows[:].rearrange("p (m t) -> p t m", t=PACK)
         )
 
-        y_codes = keep.tile([P, S], U32, align_bytes=64)
-        y_plane = keep.tile([P, S], U8, align_bytes=64)
+        y_codes = keep.tile([P, S], U32, align_bytes=ALIGN)
+        y_plane = keep.tile([P, S], U8, align_bytes=ALIGN)
         out_rows = out_0.rearrange("(p t) j -> p t j", t=PACK)
         out_words = out_1[0].rearrange("p c r -> p (c r)").bitcast(I32)
         a_sb, b_ps, best, turned, z, z_codes, z_plane, y_ps, y, y_half = [{} for i in range(10)]

@@ -25,8 +25,9 @@ TOK = 128
 TILES = S // TOK
 HALF = S // 2
 BANKS = 8
+TOP = P - 16
 ALIGN = 256
-VECTOR_MADE = 37
+VECTOR_MADE = 39
 SCALAR_MADE = 11
 
 
@@ -47,7 +48,7 @@ def tile_picked_maxsim_none_po_kernel(
         vector_made = tagged("vector_made", VECTOR_MADE)
         scalar_made = tagged("scalar_made", SCALAR_MADE)
         behind_ident = tagged("behind_ident", 2)
-        behind_rows = tagged("behind_rows", 2)
+        behind_plane = tagged("behind_plane", 2)
 
         def bank(name, shape):
             return psum.tile(shape, F32, name=name, tag="bank")
@@ -57,42 +58,45 @@ def tile_picked_maxsim_none_po_kernel(
         x_list = keep.tile([P, S // 16], U16)
         d_bytes = vector_made("d_bytes", [P, G], U8)
         nc.vector.memset(d_bytes[:].bitcast(I32), 0)
-        x_bytes = behind_rows("x_bytes", [P, T], U8)
-        nc.vector.memset(x_bytes[:].bitcast(I32), 0)
-        plane_a = vector_made("plane_a", [P, H + S], U8)
-        nc.vector.memset(plane_a[:].bitcast(I32), 0)
-        plane_b = vector_made("plane_b", [P, H], U8)
-        nc.vector.memset(plane_b[:].bitcast(I32), 0)
+        x_bytes = vector_made("x_bytes", [P, T], U8)
+        nc.vector.memset(x_bytes[0:TOP, :].bitcast(I32), 0)
+        x_plane = behind_plane("x_plane", [P, S], U8)
+        nc.vector.memset(x_plane[:].bitcast(I32), 0)
         ident = behind_ident("ident", [P, P], F32)
         nc.vector.memset(ident[:], 0.0)
         make_identity(nc, ident[:], nomemset=True)
 
+        nc.sync.dma_start(x_list[:], offs)
+        nc.sync.dma_start(x_bytes[TOP:P, :].bitcast(I32), x_scales[0].bitcast(I32))
         nc.sync.dma_start(k1_list[:], k1)
         nc.sync.dma_start(k2_list[:], k2)
-        nc.sync.dma_start(d_bytes[0:P:BLOCK, :].bitcast(I32), d_scales[0].bitcast(I32))
-        nc.sync.dma_start(x_list[:], offs)
         gain_raw = keep.tile([P, PACK], F32)
         nc.sync.dma_start(gain_raw[:], gn.rearrange("(p t) o -> p (t o)", t=PACK))
         gain = vector_made("gain", [P, PACK], F32)
         nc.scalar.mul(gain[:], gain_raw[:], 0.0625)
-        nc.sync.dma_start(x_bytes[0:P:BLOCK, :].bitcast(I32), x_scales[0].bitcast(I32))
-        d_table = behind_rows("d_table", [P, G], I32)
+        nc.sync.dma_start(d_bytes[0:P:BLOCK, :].bitcast(I32), d_scales[0].bitcast(I32))
+        d_table = behind_plane("d_table", [P, G], I32)
         nc.sync.dma_start(d_table[:], d_words[0].rearrange("p c r -> p (c r)").bitcast(I32))
         x_table = behind_ident("x_table", [P, T], I32)
         nc.sync.dma_start(x_table[:], x_words[0].rearrange("p c r -> p (c r)").bitcast(I32))
 
-        def place_rows(queue, plane, picked):
-            for r in range(QUADS):
-                queue.dma_start(plane[r:P:32, :].bitcast(I32), picked[BLOCK * r : P : 32, :].bitcast(I32))
+        x_picked = vector_made("x_picked", [P, S], U8)
+        nc.vector.tensor_copy(x_picked[:], x_bytes[:].indirect(x_list[:]))
+        for r in range(QUADS):
+            nc.scalar.dma_start(x_plane[r:P:32, :].bitcast(I32), x_picked[TOP + r : P : QUADS, :].bitcast(I32))
+        k1_picked = vector_made("k1_picked", [P, H], U8)
+        nc.vector.tensor_copy(k1_picked[:], d_bytes[:].indirect(k1_list[:]))
+        k2_picked = vector_made("k2_picked", [P, H], U8)
+        nc.vector.tensor_copy(k2_picked[:], d_bytes[:].indirect(k2_list[:]))
 
-        picked_a = vector_made("picked_a", [P, H + S], U8)
-        nc.vector.tensor_copy(picked_a[:, 0:H], d_bytes[:].indirect(k1_list[:]))
-        nc.vector.tensor_copy(picked_a[:, H:], x_bytes[:].indirect(x_list[:]))
-        place_rows(nc.scalar, plane_a, picked_a)
-        picked_b = vector_made("picked_b", [P, H], U8)
-        nc.vector.tensor_copy(picked_b[:], d_bytes[:].indirect(k2_list[:]))
-        place_rows(nc.sync, plane_b, picked_b)
+        def place_rows(picked):
+            plane = vector_made("key_plane", [P, H], U8)
+            nc.vector.tensor_copy(plane[:].bitcast(I32), picked[:].bitcast(I32))
+            for r in range(1, QUADS):
+                nc.sync.dma_start(plane[r:P:32, :].bitcast(I32), picked[BLOCK * r : P : 32, :].bitcast(I32))
+            return plane
 
+        k1_plane = place_rows(k1_picked)
         d1_codes = vector_made("d1_codes", [P, H], U32)
         nc.vector.tensor_copy(d1_codes[:], d_table[:].bitcast(U32).indirect(k1_list[:]))
         x_codes = {}
@@ -103,6 +107,7 @@ def tile_picked_maxsim_none_po_kernel(
                 x_codes[h][:], x_table[:].bitcast(U32).indirect(x_list[:, HALF // 16 * h : HALF // 16 * (h + 1)])
             )
 
+        k2_plane = place_rows(k2_picked)
         w_rows = vector_made("w_rows", [P, N], U8)
         nc.vector.memset(w_rows[:].bitcast(I32), 0)
         for r in range(QUADS):
@@ -127,17 +132,17 @@ def tile_picked_maxsim_none_po_kernel(
 
         def tokens(c):
             columns = slice(TOK * c % HALF, TOK * c % HALF + TOK)
-            return x_codes[TOK * c // HALF][:, columns].bitcast(FP8X4), plane_a[:, H + TOK * c : H + TOK * (c + 1)]
+            return x_codes[TOK * c // HALF][:, columns].bitcast(FP8X4), x_plane[:, TOK * c : TOK * (c + 1)]
 
         def score_a(c):
             a_ps = bank("a_ps", [P, H])
-            nc.tensor.matmul_mx(a_ps[:], *tokens(c), d1_codes[:].bitcast(FP8X4), plane_a[:, 0:H], start=True, stop=True)
+            nc.tensor.matmul_mx(a_ps[:], *tokens(c), d1_codes[:].bitcast(FP8X4), k1_plane[:], start=True, stop=True)
             a_sb[c] = scalar_made("a_sb", [P, PACK, P], F32)
             nc.scalar.copy(a_sb[c][:], a_ps[:].rearrange("j (p t) -> j t p", t=PACK))
 
         def score_b(c):
             b_ps[c] = bank("b_ps", [P, H])
-            nc.tensor.matmul_mx(b_ps[c][:], *tokens(c), d2_codes[:].bitcast(FP8X4), plane_b[:], start=True, stop=True)
+            nc.tensor.matmul_mx(b_ps[c][:], *tokens(c), d2_codes[:].bitcast(FP8X4), k2_plane[:], start=True, stop=True)
 
         def larger(c):
             best[c] = vector_made("best", [P, PACK, P], F32)
@@ -179,7 +184,7 @@ def tile_picked_maxsim_none_po_kernel(
 
         def warm_up():
             unread = bank("unread", [P, H])
-            nc.tensor.matmul_mx(unread[:], *tokens(3), d2_codes[:].bitcast(FP8X4), plane_b[:], start=True, stop=True)
+            nc.tensor.matmul_mx(unread[:], *tokens(3), d2_codes[:].bitcast(FP8X4), k2_plane[:], start=True, stop=True)
 
         def store(c, source, queue):
             y[c] = scalar_made("y", [P, PACK, TOK], F32)

@@ -67,7 +67,7 @@ def tile_picked_maxsim_none_po_kernel(
         make_identity(nc, ident[:], nomemset=True)
 
         nc.sync.dma_start(x_list[:], offs)
-        nc.sync.dma_start(x_bytes[TOP:P, :].bitcast(I32), x_scales[0].bitcast(I32))
+        nc.scalar.dma_start(x_bytes[TOP:P, :].bitcast(I32), x_scales[0].bitcast(I32))
         nc.sync.dma_start(k1_list[:], k1)
         nc.sync.dma_start(k2_list[:], k2)
         gain_raw = keep.tile([P, PACK], F32)
@@ -182,9 +182,11 @@ def tile_picked_maxsim_none_po_kernel(
                 )
             return result
 
-        def warm_up():
-            unread = bank("unread", [P, H])
-            nc.tensor.matmul_mx(unread[:], *tokens(3), d2_codes[:].bitcast(FP8X4), k2_plane[:], start=True, stop=True)
+        def warm_up(keys):
+            unread = bank("unread", [P, keys])
+            nc.tensor.matmul_mx(
+                unread[:], *tokens(3), d2_codes[:, 0:keys].bitcast(FP8X4), k2_plane[:, 0:keys], start=True, stop=True
+            )
 
         def store(c, source, queue):
             y[c] = scalar_made("y", [P, PACK, TOK], F32)
@@ -228,14 +230,15 @@ def tile_picked_maxsim_none_po_kernel(
         turn(1)
         larger(2)
         turn(2)
-        warm_up()
+        warm_up(H)
         weigh(0)
         larger(3)
         quantise_z(0)
         y_ps[0] = product(0)
-        store(0, y_ps[0], nc.sync)
         round_on_scalar(0)
+        store(0, y_ps[0], nc.sync)
         turn(3)
+        warm_up(TOK)
         weigh(1)
         weigh(2)
         quantise_z(1)

from contextlib import ExitStack

import concourse.mybir as mybir
from concourse.masks import make_identity

K, T, S, N, G, H = 512, 2048, 512, 512, 2048, 512
FLOPS = 2 * (2 * K * H * S) + 2 * H * N * S

F32 = mybir.dt.float32
BF16 = mybir.dt.bfloat16
I32 = mybir.dt.int32
U32 = mybir.dt.uint32
U16 = mybir.dt.uint16
U8 = mybir.dt.uint8
FP8X4 = mybir.dt.float8_e4m3fn_x4
FP4X4 = mybir.dt.float4_e2m1fn_x4
MAX = mybir.AluOpType.max
MULT = mybir.AluOpType.mult

P = 128
PACK = 4
QUADS = 4
BLOCK = 8
TOK = 128
TILES = S // TOK
HALF = S // 2
BANKS = 8
TOP = P - 16
ALIGN = 256
VECTOR_MADE = 39
SCALAR_MADE = 11


def tile_picked_maxsim_none_po_kernel(
    tc, x_words, x_scales, d_words, d_scales, gn, w1_words, w1_scales, offs, k1, k2, out_0, out_1, out_2
):
    nc = tc.nc
    with ExitStack() as ctx:
        keep = ctx.enter_context(tc.tile_pool(name="keep", bufs=1))
        psum = ctx.enter_context(tc.psum_pool(name="psum", bufs=BANKS))

        def tagged(tag, bufs):
            def make(name, shape, dtype):
                return keep.tile(shape, dtype, align_bytes=ALIGN, name=name, tag=tag, bufs=bufs)

            return make

        vector_made = tagged("vector_made", VECTOR_MADE)
        scalar_made = tagged("scalar_made", SCALAR_MADE)
        behind_ident = tagged("behind_ident", 2)
        behind_plane = tagged("behind_plane", 2)

        def bank(name, shape):
            return psum.tile(shape, F32, name=name, tag="bank")

        k1_list = keep.tile([P, H // 16], U16)
        k2_list = keep.tile([P, H // 16], U16)
        x_list = keep.tile([P, S // 16], U16)
        d_bytes = vector_made("d_bytes", [P, G], U8)
        nc.vector.memset(d_bytes[:].bitcast(I32), 0)
        x_bytes = vector_made("x_bytes", [P, T], U8)
        nc.vector.memset(x_bytes[0:TOP, :].bitcast(I32), 0)
        x_plane = behind_plane("x_plane", [P, S], U8)
        nc.vector.memset(x_plane[:].bitcast(I32), 0)
        ident = behind_ident("ident", [P, P], F32)
        nc.vector.memset(ident[:], 0.0)
        make_identity(nc, ident[:], nomemset=True)

        nc.sync.dma_start(x_list[:], offs)
        nc.scalar.dma_start(x_bytes[TOP:P, :].bitcast(I32), x_scales[0].bitcast(I32))
        nc.sync.dma_start(k1_list[:], k1)
        nc.sync.dma_start(k2_list[:], k2)
        gain_raw = keep.tile([P, PACK], F32)
        nc.sync.dma_start(gain_raw[:], gn.rearrange("(p t) o -> p (t o)", t=PACK))
        gain = vector_made("gain", [P, PACK], F32)
        nc.scalar.mul(gain[:], gain_raw[:], 0.0625)
        nc.sync.dma_start(d_bytes[0:P:BLOCK, :].bitcast(I32), d_scales[0].bitcast(I32))
        d_table = behind_plane("d_table", [P, G], I32)
        nc.sync.dma_start(d_table[:], d_words[0].rearrange("p c r -> p (c r)").bitcast(I32))
        x_table = behind_ident("x_table", [P, T], I32)
        nc.sync.dma_start(x_table[:], x_words[0].rearrange("p c r -> p (c r)").bitcast(I32))

        x_picked = vector_made("x_picked", [P, S], U8)
        nc.vector.tensor_copy(x_picked[:], x_bytes[:].indirect(x_list[:]))
        for r in range(QUADS):
            nc.scalar.dma_start(x_plane[r:P:32, :].bitcast(I32), x_picked[TOP + r : P : QUADS, :].bitcast(I32))
        k1_picked = vector_made("k1_picked", [P, H], U8)
        nc.vector.tensor_copy(k1_picked[:], d_bytes[:].indirect(k1_list[:]))
        k2_picked = vector_made("k2_picked", [P, H], U8)
        nc.vector.tensor_copy(k2_picked[:], d_bytes[:].indirect(k2_list[:]))

        def place_rows(picked):
            plane = vector_made("key_plane", [P, H], U8)
            nc.vector.tensor_copy(plane[:].bitcast(I32), picked[:].bitcast(I32))
            for r in range(1, QUADS):
                nc.sync.dma_start(plane[r:P:32, :].bitcast(I32), picked[BLOCK * r : P : 32, :].bitcast(I32))
            return plane

        k1_plane = place_rows(k1_picked)
        d1_codes = vector_made("d1_codes", [P, H], U32)
        nc.vector.tensor_copy(d1_codes[:], d_table[:].bitcast(U32).indirect(k1_list[:]))
        x_codes = {}

        def pick_words(h):
            x_codes[h] = vector_made("x_codes", [P, HALF], U32)
            nc.vector.tensor_copy(
                x_codes[h][:], x_table[:].bitcast(U32).indirect(x_list[:, HALF // 16 * h : HALF // 16 * (h + 1)])
            )

        k2_plane = place_rows(k2_picked)
        w_rows = vector_made("w_rows", [P, N], U8)
        nc.vector.memset(w_rows[:].bitcast(I32), 0)
        for r in range(QUADS):
            nc.sync.dma_start(w_rows[r:P:32, :].bitcast(I32), w1_scales[0, r:16:4, :].bitcast(I32))
        pick_words(0)
        w_raw = vector_made("w_raw", [P, 2 * N], U8)
        nc.sync.dma_start(w_raw[:].bitcast(I32), w1_words[0].bitcast(I32))
        d2_codes = vector_made("d2_codes", [P, H], U32)
        nc.vector.tensor_copy(d2_codes[:], d_table[:].bitcast(U32).indirect(k2_list[:]))
        pick_words(1)

        w_plane = vector_made("w_plane", [P, N], U8)
        nc.vector.tensor_copy(
            w_plane[:].rearrange("p (t m) -> p t m", t=PACK), w_rows[:].rearrange("p (m t) -> p t m", t=PACK)
        )

        y_codes = keep.tile([P, S], U32, align_bytes=ALIGN)
        y_plane = keep.tile([P, S], U8, align_bytes=ALIGN)
        out_rows = out_0.rearrange("(p t) j -> p t j", t=PACK)
        out_words = out_1[0].rearrange("p c r -> p (c r)").bitcast(I32)
        a_sb, b_ps, best, turned, z, z_codes, z_plane, y_ps, y, y_half = [{} for i in range(10)]

        def tokens(c):
            columns = slice(TOK * c % HALF, TOK * c % HALF + TOK)
            return x_codes[TOK * c // HALF][:, columns].bitcast(FP8X4), x_plane[:, TOK * c : TOK * (c + 1)]

        def score_a(c):
            a_ps = bank("a_ps", [P, H])
            nc.tensor.matmul_mx(a_ps[:], *tokens(c), d1_codes[:].bitcast(FP8X4), k1_plane[:], start=True, stop=True)
            a_sb[c] = scalar_made("a_sb", [P, PACK, P], F32)
            nc.scalar.copy(a_sb[c][:], a_ps[:].rearrange("j (p t) -> j t p", t=PACK))

        def score_b(c):
            b_ps[c] = bank("b_ps", [P, H])
            nc.tensor.matmul_mx(b_ps[c][:], *tokens(c), d2_codes[:].bitcast(FP8X4), k2_plane[:], start=True, stop=True)

        def larger(c):
            best[c] = vector_made("best", [P, PACK, P], F32)
            nc.vector.tensor_tensor(best[c][:], b_ps[c][:].rearrange("j (p t) -> j t p", t=PACK), a_sb[c][:], MAX)

        def turn(c, slots=range(PACK)):
            if c not in turned:
                turned[c] = bank("turned", [P, PACK, TOK])
            for t in slots:
                nc.tensor.transpose(turned[c][:, t, :], best[c][:, t, :], ident[:])

        def weigh(c):
            z[c] = vector_made("z", [P, TOK, PACK], BF16)
            nc.vector.tensor_tensor(
                z[c][:],
                turned[c][:].rearrange("p t j -> p j t"),
                gain[:].unsqueeze(1).to_broadcast([P, TOK, PACK]),
                MULT,
            )

        def quantise_z(c):
            z_codes[c] = vector_made("z_codes", [P, TOK], U32)
            z_plane[c] = keep.tile([P, TOK], U8, align_bytes=64, name="z_plane", bufs=TILES)
            nc.vector.quantize_mx(z_codes[c][:].bitcast(FP8X4), z_plane[c][:], z[c][:].rearrange("p j t -> p (j t)"))

        def product(c):
            result = bank("y_ps", [P, PACK, TOK])
            for t in range(PACK):
                nc.tensor.matmul_mx(
                    result[:, t, :],
                    w_codes[:, P * t : P * (t + 1)].bitcast(FP4X4),
                    w_plane[:, P * t : P * (t + 1)],
                    z_codes[c][:].bitcast(FP8X4),
                    z_plane[c][:],
                    start=True,
                    stop=True,
                )
            return result

        def warm_up(keys):
            unread = bank("unread", [P, keys])
            nc.tensor.matmul_mx(
                unread[:], *tokens(3), d2_codes[:, 0:keys].bitcast(FP8X4), k2_plane[:, 0:keys], start=True, stop=True
            )

        def store(c, source, queue):
            y[c] = scalar_made("y", [P, PACK, TOK], F32)
            nc.scalar.copy(y[c][:], source[:])
            queue.dma_start(out_rows[:, :, TOK * c : TOK * (c + 1)], y[c][:])

        def round_on_scalar(c):
            y_half[c] = scalar_made("y_half", [P, TOK, PACK], BF16)
            nc.scalar.copy(y_half[c][:], y_ps[c][:].rearrange("p t j -> p j t"))

        def round_on_vector(c, source):
            y_half[c] = vector_made("y_half", [P, TOK, PACK], BF16)
            nc.vector.tensor_copy(y_half[c][:], source[:].rearrange("p t j -> p j t"))

        def quantise_y(c):
            columns = slice(TOK * c, TOK * (c + 1))
            nc.vector.quantize_mx(
                y_codes[:, columns].bitcast(FP8X4), y_plane[:, columns], y_half[c][:].rearrange("p j t -> p (j t)")
            )

        def store_codes(h):
            columns = slice(HALF * h, HALF * (h + 1))
            nc.sync.dma_start(out_words[:, columns], y_codes[:, columns].bitcast(I32))

        score_a(0)
        score_a(1)
        score_b(0)
        score_a(2)
        score_b(1)
        larger(0)
        score_b(2)
        score_a(3)
        w_codes = scalar_made("w_codes", [P, N], U16)
        nc.scalar.copy(
            w_codes[:].rearrange("p (t m) -> p t m", t=PACK),
            w_raw[:].bitcast(U16).rearrange("p (m t) -> p t m", t=PACK),
        )
        turn(0)
        score_b(3)
        larger(1)
        turn(1)
        larger(2)
        turn(2)
        warm_up(H)
        weigh(0)
        larger(3)
        quantise_z(0)
        y_ps[0] = product(0)
        round_on_scalar(0)
        store(0, y_ps[0], nc.sync)
        turn(3)
        warm_up(TOK)
        weigh(1)
        weigh(2)
        quantise_z(1)
        y_ps[1] = product(1)
        store(1, y_ps[1], nc.sync)
        quantise_z(2)
        y_ps[2] = product(2)
        store(2, y_ps[2], nc.sync)
        round_on_scalar(2)
        weigh(3)
        quantise_y(0)
        quantise_z(3)
        y_ps[3] = product(3)
        store(3, product(3), nc.scalar)
        round_on_vector(1, y[1])
        quantise_y(1)
        store_codes(0)
        round_on_vector(3, y_ps[3])
        quantise_y(2)
        quantise_y(3)
        store_codes(1)
        for r in range(QUADS):
            queue = nc.scalar if r < QUADS - 1 else nc.sync
            queue.dma_start(out_2[0, r:16:4, :].bitcast(I32), y_plane[r:P:32, :].bitcast(I32))
